import numpy as np
import ml_dtypes


def mxq(x, axis, fmt="e4m3"):
    dtype, down = {"e4m3": (ml_dtypes.float8_e4m3fn, 7), "e5m2": (ml_dtypes.float8_e5m2, 14)}[fmt]
    v = np.moveaxis(np.asarray(x, np.float32).astype(ml_dtypes.bfloat16).astype(np.float64), axis, -1)
    blocks = v.reshape(v.shape[:-1] + (-1, 32))
    amax = np.abs(blocks).max(-1, keepdims=True)
    byte = np.maximum(np.where(amax > 0, np.frexp(amax)[1] - 1 + 127, 0) - down, 1)
    scale = np.exp2(byte - 127.0)
    codes = (blocks / scale).astype(np.float32).astype(dtype).astype(np.float64)
    return np.moveaxis((codes * scale).reshape(v.shape), -1, axis)


WIDE = False


def mx_kscale(k):
    if not WIDE:
        return np.ones(k)
    levels = np.array([10, -10, 5, -5, 0])
    if k % 512:
        return np.exp2(np.random.permutation(np.resize(levels, k // 32))).repeat(32)
    a = np.empty((k // 512, 16))
    for p in range(k // 512):
        a[p, :8] = np.random.permutation(np.resize(levels, 8))
        for g in range(8):
            far = levels[np.abs(levels - a[p, g]) >= 10]
            a[p, g + 8] = far[np.random.randint(len(far))]
    return np.exp2(a.ravel()).repeat(32)


def f64(x):
    return np.asarray(x).astype(np.float64)


def striped8(idx):
    return np.asarray(idx).reshape(8, -1, 16).transpose(0, 2, 1).reshape(128, -1).astype(np.uint16)


def unstriped8(offs):
    return offs.reshape(8, 16, -1).transpose(0, 2, 1).reshape(8, -1).astype(np.int64)


def pick8(x, idx, run):
    r = np.arange(len(x))
    return x[r[:, None], idx[r % (8 * run) // run]]


E2M1 = np.array([0.0, 0.5, 1.0, 1.5, 2.0, 3.0, 4.0, 6.0, -0.0, -0.5, -1.0, -1.5, -2.0, -3.0, -4.0, -6.0])


def pack_weight(w, fmt):
    k, n = w.shape
    w = f64(np.asarray(w, np.float32).astype(ml_dtypes.bfloat16)).reshape(k // 32, 32, n)
    amax = np.abs(w).max(1)
    if fmt == "e4m3":
        byte = np.frexp(amax)[1] - 1 + 127 - 7
    else:
        mant, ex = np.frexp(amax / 6.0)
        byte = np.where(mant > 0.5, ex, ex - 1) + 127
    byte = np.clip(np.where(amax > 0, byte, 1), 1, 254)
    scaled = (w * np.exp2(127.0 - byte)[:, None, :]).reshape(k, n).astype(np.float32)
    by_word = np.ascontiguousarray(scaled.reshape(k // 512, 128, 4, n).transpose(0, 1, 3, 2))
    if fmt == "e4m3":
        words = by_word.astype(ml_dtypes.float8_e4m3fn).view(np.uint8)
    else:
        c = by_word.astype(ml_dtypes.float4_e2m1fn).view(np.uint8) & 0xF
        words = (c[..., 0::2] | (c[..., 1::2] << 4)).reshape(k // 512, 128, 2 * n)
    return np.ascontiguousarray(words), np.ascontiguousarray(byte.astype(np.uint8).reshape(k // 512, 16, n))


def unpack_weight(words, scales, fmt):
    g, _, n = scales.shape
    words = np.ascontiguousarray(words).reshape(g, 128, n, -1)
    if fmt == "e4m3":
        vals = words.view(ml_dtypes.float8_e4m3fn).astype(np.float64)
    else:
        nib = np.empty((g, 128, n, 4), np.uint8)
        nib[..., 0::2] = words & 0xF
        nib[..., 1::2] = words >> 4
        vals = E2M1[nib]
    vals = vals * np.repeat(np.exp2(scales.astype(np.float64) - 127.0), 8, axis=1)[..., None]
    return vals.transpose(0, 1, 3, 2).reshape(g * 512, n)


def sigmoid(v):
    return 1.0 / (1.0 + np.exp(-v))


D, E, T, Q, I = 512, 512, 1024, 128, 512


def setup_inputs():
    n = np.random.standard_normal
    idx = np.stack([np.random.permutation(T)[:I] for _ in range(8)])
    fd = mx_kscale(D)
    fe = mx_kscale(E)
    keysp = pack_weight(n((D, T)) / fd[:, None], "e2m1")
    return {
        "query": (n((D, Q)) * 0.4 / np.sqrt(D) * fd[:, None]).astype(np.float32),
        "keys_words": keysp[0],
        "keys_scales": keysp[1],
        "gout": (n((E, Q)) * 1 / np.sqrt(E) * fe[:, None]).astype(np.float32),
        "vals": (n((E, T)) / fe[:, None]).astype(np.float32),
        "steep": (np.random.uniform(2.0, 5.0, (Q, 1))).astype(np.float32),
        "boost": (np.random.uniform(0.5, 2.0, (1, I))).astype(np.float32),
        "fac": (np.random.uniform(0.5, 2.0, (1, T))).astype(np.float32),
        "old": (0.5 * n((Q, T))).astype(np.float32),
        "offs": striped8(idx),
    }


def reference(query, keys_words, keys_scales, gout, vals, steep, boost, fac, old, offs):
    idx = unstriped8(offs)
    keysu = unpack_weight(keys_words, keys_scales, "e2m1")
    queryq = mxq(f64(query), 0, "e4m3")
    a = queryq.T @ keysu
    b = sigmoid(pick8(a, idx, 16) * f64(steep))
    bb = b * f64(boost)
    bf = np.zeros((Q, T))
    bf[np.arange(Q)[:, None], idx[np.arange(Q) % 128 // 16]] = bb
    s = a + bf
    p = np.exp(s - np.max(s, axis=1, keepdims=True))
    z = np.sum(p, axis=1, keepdims=True)
    goutq = mxq(f64(gout), 0, "e4m3")
    valsq = mxq(f64(vals), 0, "e4m3")
    c0 = goutq.T @ valsq
    dz = np.sum(c0 * p * f64(fac) / np.square(z) * (-1.0), axis=1, keepdims=True)
    dp = c0 / z * f64(fac) + dz
    ds = dp * p
    dbb = pick8(ds, idx, 16)
    db = dbb * f64(boost)
    e1 = db * b * (1.0 - b) * f64(steep)
    s1 = np.zeros((Q, T))
    s1[np.arange(Q)[:, None], idx[np.arange(Q) % 128 // 16]] = e1
    da = ds + s1
    y = da * 1024.0 + f64(old)
    return y

@@ -1,0 +1,229 @@
+import math
+from contextlib import ExitStack
+
+import concourse.mybir as mybir
+from concourse.masks import make_identity
+
+D, E, T, Q, I = 512, 512, 1024, 128, 512
+FLOPS = 2 * Q * T * (D + E)
+
+F32 = mybir.dt.float32
+BF16 = mybir.dt.bfloat16
+I32 = mybir.dt.int32
+U32 = mybir.dt.uint32
+U16 = mybir.dt.uint16
+U8 = mybir.dt.uint8
+FP8X4 = mybir.dt.float8_e4m3fn_x4
+FP4X4 = mybir.dt.float4_e2m1fn_x4
+ACT = mybir.ActivationFunctionType
+ALU = mybir.AluOpType
+
+P = 128
+PACK = 4
+BANK = 512
+CHUNK = 256
+N_CHUNKS = T // CHUNK
+OUT_SCALE = 1024.0
+
+
+def interleave(copy, grouped, raw):
+    copy(grouped.rearrange("p (c i) t -> p c t i", i=4), raw.rearrange("p t (c i) -> p c t i", i=4))
+
+
+def tile_attend_bboost_heads_kernel(tc, query, keys_words, keys_scales, gout, vals, steep, boost, fac, old, offs, out):
+    nc = tc.nc
+    with ExitStack() as ctx:
+        sb = ctx.enter_context(tc.tile_pool(name="sb", bufs=1))
+        ps = ctx.enter_context(tc.psum_pool(name="ps", bufs=1))
+
+        k_scales = sb.tile([P, T], U8, align_bytes=64)
+        nc.gpsimd.memset(k_scales[:].bitcast(I32), 0)
+        rows = sb.tile([P, P], F32)
+        nc.vector.memset(rows[:], 0.0)
+        placed = sb.tile([P, T], F32)
+        nc.vector.memset(placed[:], 0.0)
+
+        q_raw = sb.tile([P, PACK, Q], F32)
+        nc.sync.dma_start(out=q_raw[:], in_=query.rearrange("(p j) w -> p j w", j=PACK))
+        k_words = sb.tile([P, 2 * T], U8, align_bytes=64)
+        nc.sync.dma_start(out=k_words[:].bitcast(I32), in_=keys_words[0].bitcast(I32))
+        for quad in range(4):
+            nc.sync.dma_start(
+                out=k_scales[32 * quad : 32 * quad + 4, :].bitcast(I32),
+                in_=keys_scales[0, 4 * quad : 4 * quad + 4, :].bitcast(I32),
+            )
+        g_raw = sb.tile([P, PACK, Q], F32)
+        nc.sync.dma_start(out=g_raw[:], in_=gout.rearrange("(p j) w -> p j w", j=PACK))
+        vals_pj = vals.rearrange("(p j) w -> p j w", j=PACK)
+        v_raw = [sb.tile([P, PACK, CHUNK], F32, name=f"v_raw{c}", tag=f"v_raw{c}") for c in range(N_CHUNKS)]
+        nc.sync.dma_start(out=v_raw[0][:], in_=vals_pj[:, :, 0:CHUNK])
+        offsets = sb.tile([P, I // 16], U16)
+        nc.sync.dma_start(offsets[:], offs)
+        boost_cols = sb.tile([P, 4], F32)
+        nc.sync.dma_start(out=boost_cols[:], in_=boost.rearrange("o (p c) -> (o p) c", c=4))
+        steep_sb = sb.tile([P, 1], F32)
+        nc.sync.dma_start(out=steep_sb[:], in_=steep)
+        nc.sync.dma_start(out=rows[0:8, :], in_=fac.rearrange("o (c n) -> (o c) n", n=P))
+        for c in range(1, N_CHUNKS):
+            nc.sync.dma_start(out=v_raw[c][:], in_=vals_pj[:, :, c * CHUNK : (c + 1) * CHUNK])
+        old_sb = sb.tile([P, T], F32)
+        nc.sync.dma_start(out=old_sb[:], in_=old)
+        ident = sb.tile([P, P], F32)
+        make_identity(nc, ident[:])
+
+
+        q_bf = sb.tile([P, Q, PACK], BF16, align_bytes=64)
+        interleave(nc.vector.tensor_copy, q_bf[:], q_raw[:])
+        q_codes = sb.tile([P, Q], U32, align_bytes=64)
+        q_scales = sb.tile([P, Q], U8, align_bytes=64)
+        nc.vector.quantize_mx(out=q_codes[:].bitcast(FP8X4), scales=q_scales[:], in_=q_bf[:].rearrange("p w j -> p (w j)"))
+        a_sb = sb.tile([P, T], F32)
+        for c in range(N_CHUNKS):
+            cols = slice(c * CHUNK, (c + 1) * CHUNK)
+            a_ps = ps.tile([P, CHUNK], F32, tag="mm", bufs=4, name="a_ps")
+            nc.tensor.matmul_mx(
+                out=a_ps[:],
+                lhsT=q_codes[:].bitcast(FP8X4),
+                lhsT_scale=q_scales[:],
+                rhs=k_words[:, 2 * c * CHUNK : 2 * (c + 1) * CHUNK].bitcast(FP4X4),
+                rhs_scale=k_scales[:, cols],
+                start=True,
+                stop=True,
+            )
+            nc.scalar.copy(a_sb[:, cols], a_ps[:])
+
+        neg_half_steep = sb.tile([P, 1], F32)
+        nc.scalar.activation(neg_half_steep[:], steep_sb[:], ACT.Copy, scale=-0.5)
+        boost_ps = ps.tile([P, 4, P], F32, tag="late", bufs=2, name="boost_ps")
+        for c in range(4):
+            nc.tensor.transpose(boost_ps[:, c, :], boost_cols[:, c : c + 1].to_broadcast([P, P]), ident[:])
+        boost_sb = sb.tile([P, I], F32)
+        nc.scalar.copy(boost_sb[:].rearrange("p (n c) -> p n c", c=4), boost_ps[:].rearrange("p c n -> p n c"))
+        cols_ps = ps.tile([P, P], F32, tag="late", bufs=2, name="cols_ps")
+        nc.tensor.transpose(cols_ps[:], rows[:], ident[:])
+        consts = sb.tile([P, 8], F32)
+        nc.scalar.copy(consts[:], cols_ps[:, 0:8])
+
+        g_bf = sb.tile([P, Q, PACK], BF16, align_bytes=64)
+        interleave(nc.vector.tensor_copy, g_bf[:], g_raw[:])
+        g_codes = sb.tile([P, Q], U32, align_bytes=64)
+        g_scales = sb.tile([P, Q], U8, align_bytes=64)
+        nc.vector.quantize_mx(out=g_codes[:].bitcast(FP8X4), scales=g_scales[:], in_=g_bf[:].rearrange("p w j -> p (w j)"))
+
+        v_bf = [sb.tile([P, CHUNK, PACK], BF16, align_bytes=64, name=f"v_bf{c}", tag=f"v_bf{c}") for c in range(N_CHUNKS)]
+        interleave(nc.vector.tensor_copy, v_bf[0][:], v_raw[0][:])
+
+        half = I // 2
+        a_listed = sb.tile([P, I], F32)
+        th = sb.tile([P, I], F32)
+        b = sb.tile([P, I], F32)
+        for h in range(2):
+            slots = slice(h * half, (h + 1) * half)
+            nc.vector.tensor_copy(a_listed[:, slots], a_sb[:].indirect(offsets[:, h * half // 16 : (h + 1) * half // 16]))
+            nc.scalar.activation(th[:, slots], a_listed[:, slots], ACT.Tanh, scale=neg_half_steep[:])
+            nc.scalar.activation(b[:, slots], th[:, slots], ACT.Copy, scale=-0.5, bias=0.5)
+
+        c0f_ps = [ps.tile([P, BANK], F32, tag="c0f", bufs=2, name="c0f_ps") for hh in range(2)]
+
+        def values_product(c, c0t):
+            v_codes = sb.tile([P, CHUNK], U32, align_bytes=64, name=f"v_codes{c}")
+            v_scales = sb.tile([P, CHUNK], U8, align_bytes=64, name=f"v_scales{c}")
+            nc.vector.quantize_mx(out=v_codes[:].bitcast(FP8X4), scales=v_scales[:], in_=v_bf[c][:].rearrange("p w j -> p (w j)"))
+            c0t_ps = ps.tile([P, CHUNK], F32, tag="mm", bufs=4, name="c0t_ps")
+            for j in range(CHUNK // P):
+                cols = slice(j * P, (j + 1) * P)
+                nc.tensor.matmul_mx(
+                    out=c0t_ps[:, cols],
+                    lhsT=v_codes[:, cols].bitcast(FP8X4),
+                    lhsT_scale=v_scales[:, cols],
+                    rhs=g_codes[:].bitcast(FP8X4),
+                    rhs_scale=g_scales[:],
+                    start=True,
+                    stop=True,
+                )
+            for j in range(CHUNK // P):
+                cols = slice(j * P, (j + 1) * P)
+                blk = c * (CHUNK // P) + j
+                nc.scalar.activation(c0t[:, cols], c0t_ps[:, cols], ACT.Copy, scale=consts[:, blk : blk + 1])
+            for j in range(CHUNK // P):
+                blk = c * (CHUNK // P) + j
+                at = (blk % 4) * P
+                nc.tensor.transpose(c0f_ps[blk // 4][:, at : at + P], c0t[:, j * P : (j + 1) * P], ident[:])
+
+        c0t_first = sb.tile([P, CHUNK], F32)
+        values_product(0, c0t_first)
+        for h in range(2):
+            slots = slice(h * half, (h + 1) * half)
+            nc.vector.tensor_tensor(
+                placed[:].indirect(offsets[:, h * half // 16 : (h + 1) * half // 16]), b[:, slots], boost_sb[:, slots], ALU.mult
+            )
+        for c in range(1, N_CHUNKS):
+            interleave(nc.scalar.copy, v_bf[c][:], v_raw[c][:])
+        late = sb.tile([P, 3 * CHUNK + 2 * I], F32, tag="v_raw3")
+        for c in range(1, N_CHUNKS):
+            values_product(c, late[:, (c - 1) * CHUNK : c * CHUNK])
+        half_sq = late[:, 3 * CHUNK : 3 * CHUNK + I]
+        boost_steep = late[:, 3 * CHUNK + I : 3 * CHUNK + 2 * I]
+
+        s = sb.tile([P, T], F32, tag="v_bf2", align_bytes=64)
+        nc.vector.tensor_tensor(s[:], a_sb[:], placed[:], ALU.add)
+        neg_max = sb.tile([P, 1], F32)
+        neg_s = sb.tile([P, T], F32, tag="v_bf3", align_bytes=64)
+        nc.vector.tensor_scalar(neg_s[:], s[:], -1.0, None, ALU.mult, ALU.min, accum_out=neg_max[:])
+
+        nc.scalar.activation(half_sq, th[:], ACT.Square, scale=math.sqrt(0.5))
+        nc.scalar.activation(boost_steep, boost_sb[:], ACT.Copy, scale=neg_half_steep[:])
+        slope = sb.tile([P, I], F32, tag="v_bf2", align_bytes=64)
+        nc.vector.scalar_tensor_tensor(slope[:], half_sq, 0.5, boost_steep, ALU.subtract, ALU.mult)
+
+        p = sb.tile([P, T], F32)
+        u = sb.tile([P, T], F32)
+        z_parts = [sb.tile([P, 1], F32, name=f"z{h}") for h in range(2)]
+        u_parts = [sb.tile([P, 1], F32, name=f"u{h}") for h in range(2)]
+        halves = [slice(h * BANK, (h + 1) * BANK) for h in range(2)]
+        for h in range(2):
+            nc.scalar.activation(p[:, halves[h]], neg_s[:, halves[h]], ACT.Exp, bias=neg_max[:], scale=-1.0, accum_out=z_parts[h][:])
+        nc.vector.scalar_tensor_tensor(
+            u[:, halves[0]], c0f_ps[0][:], 1.0, p[:, halves[0]], ALU.mult, ALU.mult, accum_out=u_parts[0][:]
+        )
+        z = sb.tile([P, 1], F32)
+        nc.vector.tensor_tensor(z[:], z_parts[0][:], z_parts[1][:], ALU.add)
+        rz = sb.tile([P, 1], F32)
+        nc.vector.reciprocal(rz[:], z[:])
+        nc.vector.scalar_tensor_tensor(
+            u[:, halves[1]], c0f_ps[1][:], 1.0, p[:, halves[1]], ALU.mult, ALU.mult, accum_out=u_parts[1][:]
+        )
+        mean = sb.tile([P, 1], F32)
+        nc.vector.tensor_scalar(mean[:], u_parts[0][:], u_parts[1][:], rz[:], ALU.add, ALU.mult)
+        pn = sb.tile([P, T], F32)
+        ds = sb.tile([P, T], F32)
+        for h in range(2):
+            nc.scalar.activation(pn[:, halves[h]], p[:, halves[h]], ACT.Copy, scale=rz[:])
+            nc.vector.scalar_tensor_tensor(ds[:, halves[h]], c0f_ps[h][:], mean[:], pn[:, halves[h]], ALU.subtract, ALU.mult)
+
+        ds_listed = sb.tile([P, I], F32)
+        nc.vector.tensor_copy(ds_listed[:], ds[:].indirect(offsets[:]))
+        nc.vector.tensor_tensor(placed[:].indirect(offsets[:]), ds_listed[:], slope[:], ALU.mult)
+
+        ds_scaled = sb.tile([P, T], F32)
+        dense_t = sb.tile([P, T], F32)
+        res = sb.tile([P, T], F32)
+        for h in range(2):
+            nc.scalar.activation(ds_scaled[:, halves[h]], ds[:, halves[h]], ACT.Copy, scale=OUT_SCALE)
+            sum_ps = ps.tile([P, BANK], F32, tag="mm", bufs=4, name="sum_ps")
+            for j in range(4):
+                src = slice(h * BANK + j * P, h * BANK + (j + 1) * P)
+                dst = sum_ps[:, j * P : (j + 1) * P]
+                nc.tensor.matmul(dst, old_sb[:, src], ident[:], start=True, stop=False, is_transpose=True)
+                nc.tensor.matmul(dst, ds_scaled[:, src], ident[:], start=False, stop=True, is_transpose=True)
+            nc.scalar.copy(dense_t[:, halves[h]], sum_ps[:])
+            dense_ps = ps.tile([P, BANK], F32, tag="late", bufs=2, name="dense_ps")
+            for j in range(4):
+                src = slice(h * BANK + j * P, h * BANK + (j + 1) * P)
+                nc.tensor.transpose(dense_ps[:, j * P : (j + 1) * P], dense_t[:, src], ident[:])
+            for j in range(2):
+                cols = slice(h * BANK + j * CHUNK, h * BANK + (j + 1) * CHUNK)
+                nc.vector.scalar_tensor_tensor(
+                    res[:, cols], placed[:, cols], OUT_SCALE, dense_ps[:, j * CHUNK : (j + 1) * CHUNK], ALU.mult, ALU.add
+                )
+                nc.sync.dma_start(out=out[:, cols], in_=res[:, cols])

@@ -1,4 +1,3 @@
-import math
 from contextlib import ExitStack
 
 import concourse.mybir as mybir
@@ -21,25 +20,34 @@ ALU = mybir.AluOpType
 P = 128
 PACK = 4
 BANK = 512
-CHUNK = 256
-N_CHUNKS = T // CHUNK
 OUT_SCALE = 1024.0
+SCORE_PIECES = ((0, 512), (512, 768), (768, 896), (896, 1024))
+VALUE_CHUNKS = ((0, 256), (256, 512), (512, 768), (768, 1024))
+OUT_PIECE = 256
 
 
 def interleave(copy, grouped, raw):
     copy(grouped.rearrange("p (c i) t -> p c t i", i=4), raw.rearrange("p t (c i) -> p c t i", i=4))
 
 
+def quantize(nc, codes, scales, grouped):
+    nc.vector.quantize_mx(out=codes.bitcast(FP8X4), scales=scales, in_=grouped.rearrange("p w j -> p (w j)"))
+
+
 def tile_attend_bboost_heads_kernel(tc, query, keys_words, keys_scales, gout, vals, steep, boost, fac, old, offs, out):
     nc = tc.nc
+    last = len(VALUE_CHUNKS) - 1
+    token_halves = [slice(0, BANK), slice(BANK, T)]
+    slot_halves = [slice(0, I // 2), slice(I // 2, I)]
+    list_halves = [slice(0, I // 32), slice(I // 32, I // 16)]
     with ExitStack() as ctx:
         sb = ctx.enter_context(tc.tile_pool(name="sb", bufs=1))
         ps = ctx.enter_context(tc.psum_pool(name="ps", bufs=1))
 
         k_scales = sb.tile([P, T], U8, align_bytes=64)
         nc.gpsimd.memset(k_scales[:].bitcast(I32), 0)
-        rows = sb.tile([P, P], F32)
-        nc.vector.memset(rows[:], 0.0)
+        fac_rows = sb.tile([P, P], F32)
+        nc.vector.memset(fac_rows[:], 0.0)
         placed = sb.tile([P, T], F32)
         nc.vector.memset(placed[:], 0.0)
 
@@ -54,176 +62,184 @@ def tile_attend_bboost_heads_kernel(tc, query, keys_words, keys_scales, gout, va
             )
         g_raw = sb.tile([P, PACK, Q], F32)
         nc.sync.dma_start(out=g_raw[:], in_=gout.rearrange("(p j) w -> p j w", j=PACK))
-        vals_pj = vals.rearrange("(p j) w -> p j w", j=PACK)
-        v_raw = [sb.tile([P, PACK, CHUNK], F32, name=f"v_raw{c}", tag=f"v_raw{c}") for c in range(N_CHUNKS)]
-        nc.sync.dma_start(out=v_raw[0][:], in_=vals_pj[:, :, 0:CHUNK])
-        offsets = sb.tile([P, I // 16], U16)
-        nc.sync.dma_start(offsets[:], offs)
         boost_cols = sb.tile([P, 4], F32)
         nc.sync.dma_start(out=boost_cols[:], in_=boost.rearrange("o (p c) -> (o p) c", c=4))
+        offsets = sb.tile([P, I // 16], U16)
+        nc.sync.dma_start(offsets[:], offs)
         steep_sb = sb.tile([P, 1], F32)
         nc.sync.dma_start(out=steep_sb[:], in_=steep)
-        nc.sync.dma_start(out=rows[0:8, :], in_=fac.rearrange("o (c n) -> (o c) n", n=P))
-        for c in range(1, N_CHUNKS):
-            nc.sync.dma_start(out=v_raw[c][:], in_=vals_pj[:, :, c * CHUNK : (c + 1) * CHUNK])
+        vals_pj = vals.rearrange("(p j) w -> p j w", j=PACK)
+        v_raw = []
+        for c, (lo, hi) in enumerate(VALUE_CHUNKS):
+            raw = sb.tile([P, PACK, hi - lo], F32, name=f"v_raw{c}", tag=f"v_raw{c}")
+            nc.sync.dma_start(out=raw[:], in_=vals_pj[:, :, lo:hi])
+            v_raw.append(raw)
+            if c == 1:
+                nc.sync.dma_start(out=fac_rows[0 : T // P, :], in_=fac.rearrange("o (c n) -> (o c) n", n=P))
         old_sb = sb.tile([P, T], F32)
         nc.sync.dma_start(out=old_sb[:], in_=old)
         ident = sb.tile([P, P], F32)
         make_identity(nc, ident[:])
 
+        neg_half_steep = sb.tile([P, 1], F32)
+        nc.gpsimd.tensor_scalar(neg_half_steep[:], steep_sb[:], -0.5, 0.0, ALU.mult, ALU.add)
+        neg_steep_scaled = sb.tile([P, 1], F32)
+        nc.gpsimd.tensor_scalar(neg_steep_scaled[:], steep_sb[:], -OUT_SCALE, 0.0, ALU.mult, ALU.add)
 
         q_bf = sb.tile([P, Q, PACK], BF16, align_bytes=64)
-        interleave(nc.vector.tensor_copy, q_bf[:], q_raw[:])
         q_codes = sb.tile([P, Q], U32, align_bytes=64)
         q_scales = sb.tile([P, Q], U8, align_bytes=64)
-        nc.vector.quantize_mx(out=q_codes[:].bitcast(FP8X4), scales=q_scales[:], in_=q_bf[:].rearrange("p w j -> p (w j)"))
-        a_sb = sb.tile([P, T], F32)
-        for c in range(N_CHUNKS):
-            cols = slice(c * CHUNK, (c + 1) * CHUNK)
-            a_ps = ps.tile([P, CHUNK], F32, tag="mm", bufs=4, name="a_ps")
+        q_halves = [slice(0, Q // 2), slice(Q // 2, Q)]
+        for cols in q_halves:
+            interleave(nc.vector.tensor_copy, q_bf[:, cols, :], q_raw[:, :, cols])
+        for cols in q_halves:
+            quantize(nc, q_codes[:, cols], q_scales[:, cols], q_bf[:, cols, :])
+        a = sb.tile([P, T], F32)
+        for c, (lo, hi) in enumerate(SCORE_PIECES):
+            a_ps = ps.tile([P, hi - lo], F32, tag="mm", bufs=4, name="a_ps")
             nc.tensor.matmul_mx(
                 out=a_ps[:],
                 lhsT=q_codes[:].bitcast(FP8X4),
                 lhsT_scale=q_scales[:],
-                rhs=k_words[:, 2 * c * CHUNK : 2 * (c + 1) * CHUNK].bitcast(FP4X4),
-                rhs_scale=k_scales[:, cols],
+                rhs=k_words[:, 2 * lo : 2 * hi].bitcast(FP4X4),
+                rhs_scale=k_scales[:, lo:hi],
                 start=True,
                 stop=True,
             )
-            nc.scalar.copy(a_sb[:, cols], a_ps[:])
+            copy_out = nc.vector.tensor_copy if c % 2 else nc.scalar.copy
+            copy_out(a[:, lo:hi], a_ps[:])
 
-        neg_half_steep = sb.tile([P, 1], F32)
-        nc.scalar.activation(neg_half_steep[:], steep_sb[:], ACT.Copy, scale=-0.5)
-        boost_ps = ps.tile([P, 4, P], F32, tag="late", bufs=2, name="boost_ps")
+        boost_ps = ps.tile([P, 4, P], F32, tag="mm", bufs=4, name="boost_ps")
         for c in range(4):
             nc.tensor.transpose(boost_ps[:, c, :], boost_cols[:, c : c + 1].to_broadcast([P, P]), ident[:])
-        boost_sb = sb.tile([P, I], F32)
-        nc.scalar.copy(boost_sb[:].rearrange("p (n c) -> p n c", c=4), boost_ps[:].rearrange("p c n -> p n c"))
-        cols_ps = ps.tile([P, P], F32, tag="late", bufs=2, name="cols_ps")
-        nc.tensor.transpose(cols_ps[:], rows[:], ident[:])
-        consts = sb.tile([P, 8], F32)
-        nc.scalar.copy(consts[:], cols_ps[:, 0:8])
 
         g_bf = sb.tile([P, Q, PACK], BF16, align_bytes=64)
         interleave(nc.vector.tensor_copy, g_bf[:], g_raw[:])
         g_codes = sb.tile([P, Q], U32, align_bytes=64)
         g_scales = sb.tile([P, Q], U8, align_bytes=64)
-        nc.vector.quantize_mx(out=g_codes[:].bitcast(FP8X4), scales=g_scales[:], in_=g_bf[:].rearrange("p w j -> p (w j)"))
+        quantize(nc, g_codes[:], g_scales[:], g_bf[:])
 
-        v_bf = [sb.tile([P, CHUNK, PACK], BF16, align_bytes=64, name=f"v_bf{c}", tag=f"v_bf{c}") for c in range(N_CHUNKS)]
-        interleave(nc.vector.tensor_copy, v_bf[0][:], v_raw[0][:])
-
-        half = I // 2
         a_listed = sb.tile([P, I], F32)
-        th = sb.tile([P, I], F32)
         b = sb.tile([P, I], F32)
-        for h in range(2):
-            slots = slice(h * half, (h + 1) * half)
-            nc.vector.tensor_copy(a_listed[:, slots], a_sb[:].indirect(offsets[:, h * half // 16 : (h + 1) * half // 16]))
-            nc.scalar.activation(th[:, slots], a_listed[:, slots], ACT.Tanh, scale=neg_half_steep[:])
-            nc.scalar.activation(b[:, slots], th[:, slots], ACT.Copy, scale=-0.5, bias=0.5)
+        for slots, entries in zip(slot_halves, list_halves):
+            nc.vector.tensor_copy(a_listed[:, slots], a[:].indirect(offsets[:, entries]))
+            th = sb.tile([P, I // 2], F32, tag="v_bf0", align_bytes=64)
+            nc.scalar.activation(th[:], a_listed[:, slots], ACT.Tanh, scale=neg_half_steep[:])
+            nc.scalar.activation(b[:, slots], th[:], ACT.Copy, scale=-0.5, bias=0.5)
+        boost_sb = sb.tile([P, I], F32)
+        nc.vector.tensor_copy(boost_sb[:].rearrange("p (n c) -> p n c", c=4), boost_ps[:].rearrange("p c n -> p n c"))
+        for slots, entries in zip(slot_halves, list_halves):
+            nc.vector.tensor_tensor(placed[:].indirect(offsets[:, entries]), b[:, slots], boost_sb[:, slots], ALU.mult)
 
-        c0f_ps = [ps.tile([P, BANK], F32, tag="c0f", bufs=2, name="c0f_ps") for hh in range(2)]
-
-        def values_product(c, c0t):
-            v_codes = sb.tile([P, CHUNK], U32, align_bytes=64, name=f"v_codes{c}")
-            v_scales = sb.tile([P, CHUNK], U8, align_bytes=64, name=f"v_scales{c}")
-            nc.vector.quantize_mx(out=v_codes[:].bitcast(FP8X4), scales=v_scales[:], in_=v_bf[c][:].rearrange("p w j -> p (w j)"))
-            c0t_ps = ps.tile([P, CHUNK], F32, tag="mm", bufs=4, name="c0t_ps")
-            for j in range(CHUNK // P):
-                cols = slice(j * P, (j + 1) * P)
+        v_bf = []
+        for c, (lo, hi) in enumerate(VALUE_CHUNKS):
+            grouped = sb.tile([P, hi - lo, PACK], BF16, align_bytes=64, name=f"v_bf{c}", tag=f"v_bf{c}")
+            interleave(nc.scalar.copy, grouped[:], v_raw[c][:])
+            v_bf.append(grouped)
+        fac_ps = ps.tile([P, P], F32, tag="late", bufs=2, name="fac_ps")
+        nc.tensor.transpose(fac_ps[:], fac_rows[:], ident[:])
+        after_casts = sb.tile([P, T + T // P], F32, tag=f"v_raw{last}")
+        c0f_t = after_casts[:, 0:T]
+        fac_cols = after_casts[:, T : T + T // P]
+        nc.scalar.copy(fac_cols, fac_ps[:, 0 : T // P])
+        c0f_ps = [ps.tile([P, BANK], F32, tag="c0f", bufs=2, name="c0f_ps") for cols in token_halves]
+        for c, (lo, hi) in enumerate(VALUE_CHUNKS):
+            v_codes = sb.tile([P, hi - lo], U32, align_bytes=64, name=f"v_codes{c}")
+            v_scales = sb.tile([P, hi - lo], U8, align_bytes=64, name=f"v_scales{c}")
+            quantize(nc, v_codes[:], v_scales[:], v_bf[c][:])
+            c0_t_ps = ps.tile([P, hi - lo], F32, tag="mm", bufs=4, name="c0_t_ps")
+            for t0 in range(lo, hi, P):
                 nc.tensor.matmul_mx(
-                    out=c0t_ps[:, cols],
-                    lhsT=v_codes[:, cols].bitcast(FP8X4),
-                    lhsT_scale=v_scales[:, cols],
+                    out=c0_t_ps[:, t0 - lo : t0 - lo + P],
+                    lhsT=v_codes[:, t0 - lo : t0 - lo + P].bitcast(FP8X4),
+                    lhsT_scale=v_scales[:, t0 - lo : t0 - lo + P],
                     rhs=g_codes[:].bitcast(FP8X4),
                     rhs_scale=g_scales[:],
                     start=True,
                     stop=True,
                 )
-            for j in range(CHUNK // P):
-                cols = slice(j * P, (j + 1) * P)
-                blk = c * (CHUNK // P) + j
-                nc.scalar.activation(c0t[:, cols], c0t_ps[:, cols], ACT.Copy, scale=consts[:, blk : blk + 1])
-            for j in range(CHUNK // P):
-                blk = c * (CHUNK // P) + j
-                at = (blk % 4) * P
-                nc.tensor.transpose(c0f_ps[blk // 4][:, at : at + P], c0t[:, j * P : (j + 1) * P], ident[:])
-
-        c0t_first = sb.tile([P, CHUNK], F32)
-        values_product(0, c0t_first)
-        for h in range(2):
-            slots = slice(h * half, (h + 1) * half)
-            nc.vector.tensor_tensor(
-                placed[:].indirect(offsets[:, h * half // 16 : (h + 1) * half // 16]), b[:, slots], boost_sb[:, slots], ALU.mult
-            )
-        for c in range(1, N_CHUNKS):
-            interleave(nc.scalar.copy, v_bf[c][:], v_raw[c][:])
-        late = sb.tile([P, 3 * CHUNK + 2 * I], F32, tag="v_raw3")
-        for c in range(1, N_CHUNKS):
-            values_product(c, late[:, (c - 1) * CHUNK : c * CHUNK])
-        half_sq = late[:, 3 * CHUNK : 3 * CHUNK + I]
-        boost_steep = late[:, 3 * CHUNK + I : 3 * CHUNK + 2 * I]
+            for t0 in range(lo, hi, P):
+                nc.scalar.activation(
+                    c0f_t[:, t0 : t0 + P], c0_t_ps[:, t0 - lo : t0 - lo + P], ACT.Copy, scale=fac_cols[:, t0 // P : t0 // P + 1]
+                )
+            for t0 in range(lo, hi, P):
+                nc.tensor.transpose(c0f_ps[t0 // BANK][:, t0 % BANK : t0 % BANK + P], c0f_t[:, t0 : t0 + P], ident[:])
 
         s = sb.tile([P, T], F32, tag="v_bf2", align_bytes=64)
-        nc.vector.tensor_tensor(s[:], a_sb[:], placed[:], ALU.add)
+        nc.vector.tensor_tensor(s[:], a[:], placed[:], ALU.add)
+        after_quant = sb.tile([P, T + I], F32, tag=f"v_bf{last}", align_bytes=64)
+        neg_s = after_quant[:, 0:T]
+        first, second = token_halves
+        neg_max_first = sb.tile([P, 1], F32)
         neg_max = sb.tile([P, 1], F32)
-        neg_s = sb.tile([P, T], F32, tag="v_bf3", align_bytes=64)
-        nc.vector.tensor_scalar(neg_s[:], s[:], -1.0, None, ALU.mult, ALU.min, accum_out=neg_max[:])
+        nc.vector.tensor_scalar(neg_s[:, first], s[:, first], -1.0, None, ALU.mult, ALU.min, accum_out=neg_max_first[:])
+        nc.vector.tensor_scalar(neg_s[:, second], s[:, second], -1.0, neg_max_first[:], ALU.mult, ALU.min, accum_out=neg_max[:])
 
-        nc.scalar.activation(half_sq, th[:], ACT.Square, scale=math.sqrt(0.5))
-        nc.scalar.activation(boost_steep, boost_sb[:], ACT.Copy, scale=neg_half_steep[:])
-        slope = sb.tile([P, I], F32, tag="v_bf2", align_bytes=64)
-        nc.vector.scalar_tensor_tensor(slope[:], half_sq, 0.5, boost_steep, ALU.subtract, ALU.mult)
+        one_minus_b = after_quant[:, T : T + I]
+        nc.gpsimd.tensor_scalar(one_minus_b, b[:], -1.0, neg_steep_scaled[:], ALU.add, ALU.mult)
+        sigmoid_slope = sb.tile([P, I], F32)
+        nc.gpsimd.tensor_tensor(sigmoid_slope[:], one_minus_b, b[:], ALU.mult)
+        slope = sb.tile([P, I], F32)
+        nc.gpsimd.tensor_tensor(slope[:], sigmoid_slope[:], boost_sb[:], ALU.mult)
 
         p = sb.tile([P, T], F32)
-        u = sb.tile([P, T], F32)
-        z_parts = [sb.tile([P, 1], F32, name=f"z{h}") for h in range(2)]
-        u_parts = [sb.tile([P, 1], F32, name=f"u{h}") for h in range(2)]
-        halves = [slice(h * BANK, (h + 1) * BANK) for h in range(2)]
-        for h in range(2):
-            nc.scalar.activation(p[:, halves[h]], neg_s[:, halves[h]], ACT.Exp, bias=neg_max[:], scale=-1.0, accum_out=z_parts[h][:])
-        nc.vector.scalar_tensor_tensor(
-            u[:, halves[0]], c0f_ps[0][:], 1.0, p[:, halves[0]], ALU.mult, ALU.mult, accum_out=u_parts[0][:]
-        )
-        z = sb.tile([P, 1], F32)
-        nc.vector.tensor_tensor(z[:], z_parts[0][:], z_parts[1][:], ALU.add)
+        z_first = sb.tile([P, 1], F32)
+        z_second = sb.tile([P, 1], F32)
+        shift = sb.tile([P, 1], F32)
+        nc.scalar.activation(p[:, first], neg_s[:, first], ACT.Exp, bias=neg_max_first[:], scale=-1.0, accum_out=z_first[:])
+        nc.scalar.activation(shift[:], neg_max_first[:], ACT.Exp, bias=neg_max[:], scale=-1.0)
+        nc.scalar.activation(p[:, second], neg_s[:, second], ACT.Exp, bias=neg_max[:], scale=-1.0, accum_out=z_second[:])
+        z = sb.tile([P, 1], F32, tag="z")
+        nc.scalar.activation(z[:], z_first[:], ACT.Identity, bias=z_second[:], scale=shift[:])
+
+        u_first = sb.tile([P, BANK], F32)
+        sum_first = sb.tile([P, 1], F32)
+        nc.vector.scalar_tensor_tensor(u_first[:], c0f_ps[0][:], 1.0, p[:, first], ALU.mult, ALU.mult, accum_out=sum_first[:])
+        sum_first_shifted = sb.tile([P, 1], F32)
+        nc.vector.tensor_tensor(sum_first_shifted[:], sum_first[:], shift[:], ALU.mult)
         rz = sb.tile([P, 1], F32)
         nc.vector.reciprocal(rz[:], z[:])
-        nc.vector.scalar_tensor_tensor(
-            u[:, halves[1]], c0f_ps[1][:], 1.0, p[:, halves[1]], ALU.mult, ALU.mult, accum_out=u_parts[1][:]
-        )
+        u_second = sb.tile([P, BANK], F32, tag="z")
+        sum_second = sb.tile([P, 1], F32)
+        nc.vector.scalar_tensor_tensor(u_second[:], c0f_ps[1][:], 1.0, p[:, second], ALU.mult, ALU.mult, accum_out=sum_second[:])
+        rz_first = sb.tile([P, 1], F32)
+        nc.vector.tensor_tensor(rz_first[:], rz[:], shift[:], ALU.mult)
         mean = sb.tile([P, 1], F32)
-        nc.vector.tensor_scalar(mean[:], u_parts[0][:], u_parts[1][:], rz[:], ALU.add, ALU.mult)
+        nc.vector.tensor_scalar(mean[:], sum_first_shifted[:], sum_second[:], rz[:], ALU.add, ALU.mult)
         pn = sb.tile([P, T], F32)
         ds = sb.tile([P, T], F32)
-        for h in range(2):
-            nc.scalar.activation(pn[:, halves[h]], p[:, halves[h]], ACT.Copy, scale=rz[:])
-            nc.vector.scalar_tensor_tensor(ds[:, halves[h]], c0f_ps[h][:], mean[:], pn[:, halves[h]], ALU.subtract, ALU.mult)
+        for h, norm in ((1, rz), (0, rz_first)):
+            cols = token_halves[h]
+            nc.scalar.activation(pn[:, cols], p[:, cols], ACT.Copy, scale=norm[:])
+            nc.vector.scalar_tensor_tensor(ds[:, cols], c0f_ps[h][:], mean[:], pn[:, cols], ALU.subtract, ALU.mult)
 
         ds_listed = sb.tile([P, I], F32)
         nc.vector.tensor_copy(ds_listed[:], ds[:].indirect(offsets[:]))
         nc.vector.tensor_tensor(placed[:].indirect(offsets[:]), ds_listed[:], slope[:], ALU.mult)
 
+        sum_ps = [ps.tile([P, BANK], F32, tag="mm", bufs=4, name="sum_ps") for cols in token_halves]
+        for t0 in range(0, T, P):
+            at = t0 % BANK
+            nc.tensor.matmul(
+                sum_ps[t0 // BANK][:, at : at + P], old_sb[:, t0 : t0 + P], ident[:], start=at == 0, stop=False, is_transpose=True
+            )
         ds_scaled = sb.tile([P, T], F32)
         dense_t = sb.tile([P, T], F32)
         res = sb.tile([P, T], F32)
-        for h in range(2):
-            nc.scalar.activation(ds_scaled[:, halves[h]], ds[:, halves[h]], ACT.Copy, scale=OUT_SCALE)
-            sum_ps = ps.tile([P, BANK], F32, tag="mm", bufs=4, name="sum_ps")
-            for j in range(4):
-                src = slice(h * BANK + j * P, h * BANK + (j + 1) * P)
-                dst = sum_ps[:, j * P : (j + 1) * P]
-                nc.tensor.matmul(dst, old_sb[:, src], ident[:], start=True, stop=False, is_transpose=True)
-                nc.tensor.matmul(dst, ds_scaled[:, src], ident[:], start=False, stop=True, is_transpose=True)
-            nc.scalar.copy(dense_t[:, halves[h]], sum_ps[:])
-            dense_ps = ps.tile([P, BANK], F32, tag="late", bufs=2, name="dense_ps")
-            for j in range(4):
-                src = slice(h * BANK + j * P, h * BANK + (j + 1) * P)
-                nc.tensor.transpose(dense_ps[:, j * P : (j + 1) * P], dense_t[:, src], ident[:])
-            for j in range(2):
-                cols = slice(h * BANK + j * CHUNK, h * BANK + (j + 1) * CHUNK)
-                nc.vector.scalar_tensor_tensor(
-                    res[:, cols], placed[:, cols], OUT_SCALE, dense_ps[:, j * CHUNK : (j + 1) * CHUNK], ALU.mult, ALU.add
+        for h in (1, 0):
+            cols = token_halves[h]
+            nc.scalar.activation(ds_scaled[:, cols], ds[:, cols], ACT.Copy, scale=OUT_SCALE)
+            for at in range(0, BANK, P):
+                t0 = h * BANK + at
+                nc.tensor.matmul(
+                    sum_ps[h][:, at : at + P], ds_scaled[:, t0 : t0 + P], ident[:], start=False, stop=at == BANK - P, is_transpose=True
                 )
-                nc.sync.dma_start(out=out[:, cols], in_=res[:, cols])
+            nc.scalar.copy(dense_t[:, cols], sum_ps[h][:])
+            dense_ps = ps.tile([P, BANK], F32, tag="late", bufs=2, name="dense_ps")
+            for at in range(0, BANK, P):
+                t0 = h * BANK + at
+                nc.tensor.transpose(dense_ps[:, at : at + P], dense_t[:, t0 : t0 + P], ident[:])
+            for at in range(0, BANK, OUT_PIECE):
+                piece = slice(h * BANK + at, h * BANK + at + OUT_PIECE)
+                nc.vector.tensor_tensor(res[:, piece], dense_ps[:, at : at + OUT_PIECE], placed[:, piece], ALU.add)
+                nc.sync.dma_start(out=out[:, piece], in_=res[:, piece])

@@ -21,7 +21,7 @@ P = 128
 PACK = 4
 BANK = 512
 OUT_SCALE = 1024.0
-SCORE_PIECES = ((0, 512), (512, 768), (768, 896), (896, 1024))
+SCORE_PIECES = ((0, 256), (256, 512), (512, 768), (768, 1024))
 VALUE_CHUNKS = ((0, 256), (256, 512), (512, 768), (768, 1024))
 OUT_PIECE = 256
 
@@ -53,6 +53,8 @@ def tile_attend_bboost_heads_kernel(tc, query, keys_words, keys_scales, gout, va
 
         q_raw = sb.tile([P, PACK, Q], F32)
         nc.sync.dma_start(out=q_raw[:], in_=query.rearrange("(p j) w -> p j w", j=PACK))
+        boost_cols = sb.tile([P, 4], F32)
+        nc.sync.dma_start(out=boost_cols[:], in_=boost.rearrange("o (p c) -> (o p) c", c=4))
         k_words = sb.tile([P, 2 * T], U8, align_bytes=64)
         nc.sync.dma_start(out=k_words[:].bitcast(I32), in_=keys_words[0].bitcast(I32))
         for quad in range(4):
@@ -62,8 +64,6 @@ def tile_attend_bboost_heads_kernel(tc, query, keys_words, keys_scales, gout, va
             )
         g_raw = sb.tile([P, PACK, Q], F32)
         nc.sync.dma_start(out=g_raw[:], in_=gout.rearrange("(p j) w -> p j w", j=PACK))
-        boost_cols = sb.tile([P, 4], F32)
-        nc.sync.dma_start(out=boost_cols[:], in_=boost.rearrange("o (p c) -> (o p) c", c=4))
         offsets = sb.tile([P, I // 16], U16)
         nc.sync.dma_start(offsets[:], offs)
         steep_sb = sb.tile([P, 1], F32)
@@ -84,9 +84,9 @@ def tile_attend_bboost_heads_kernel(tc, query, keys_words, keys_scales, gout, va
         neg_half_steep = sb.tile([P, 1], F32)
         nc.gpsimd.tensor_scalar(neg_half_steep[:], steep_sb[:], -0.5, 0.0, ALU.mult, ALU.add)
         neg_steep_scaled = sb.tile([P, 1], F32)
-        nc.gpsimd.tensor_scalar(neg_steep_scaled[:], steep_sb[:], -OUT_SCALE, 0.0, ALU.mult, ALU.add)
+        nc.gpsimd.tensor_scalar(neg_steep_scaled[:], steep_sb[:], -0.25 * OUT_SCALE, 0.0, ALU.mult, ALU.add)
 
-        q_bf = sb.tile([P, Q, PACK], BF16, align_bytes=64)
+        q_bf = sb.tile([P, Q, PACK], BF16, tag="q_bf", align_bytes=64)
         q_codes = sb.tile([P, Q], U32, align_bytes=64)
         q_scales = sb.tile([P, Q], U8, align_bytes=64)
         q_halves = [slice(0, Q // 2), slice(Q // 2, Q)]
@@ -94,9 +94,9 @@ def tile_attend_bboost_heads_kernel(tc, query, keys_words, keys_scales, gout, va
             interleave(nc.vector.tensor_copy, q_bf[:, cols, :], q_raw[:, :, cols])
         for cols in q_halves:
             quantize(nc, q_codes[:, cols], q_scales[:, cols], q_bf[:, cols, :])
-        a = sb.tile([P, T], F32)
+        a = sb.tile([P, T], F32, tag="a")
         for c, (lo, hi) in enumerate(SCORE_PIECES):
-            a_ps = ps.tile([P, hi - lo], F32, tag="mm", bufs=4, name="a_ps")
+            a_ps = ps.tile([P, hi - lo], F32, tag=f"bank{c}", name="a_ps")
             nc.tensor.matmul_mx(
                 out=a_ps[:],
                 lhsT=q_codes[:].bitcast(FP8X4),
@@ -106,12 +106,13 @@ def tile_attend_bboost_heads_kernel(tc, query, keys_words, keys_scales, gout, va
                 start=True,
                 stop=True,
             )
-            copy_out = nc.vector.tensor_copy if c % 2 else nc.scalar.copy
-            copy_out(a[:, lo:hi], a_ps[:])
+            nc.scalar.copy(a[:, lo:hi], a_ps[:])
 
-        boost_ps = ps.tile([P, 4, P], F32, tag="mm", bufs=4, name="boost_ps")
+        boost_held = sb.tile([P, 4], F32, tag="q_bf", align_bytes=64)
+        nc.vector.tensor_copy(boost_held[:], boost_cols[:])
+        boost_ps = ps.tile([P, 4, P], F32, tag="late", bufs=2, name="boost_ps")
         for c in range(4):
-            nc.tensor.transpose(boost_ps[:, c, :], boost_cols[:, c : c + 1].to_broadcast([P, P]), ident[:])
+            nc.tensor.transpose(boost_ps[:, c, :], boost_held[:, c : c + 1].to_broadcast([P, P]), ident[:])
 
         g_bf = sb.tile([P, Q, PACK], BF16, align_bytes=64)
         interleave(nc.vector.tensor_copy, g_bf[:], g_raw[:])
@@ -119,38 +120,41 @@ def tile_attend_bboost_heads_kernel(tc, query, keys_words, keys_scales, gout, va
         g_scales = sb.tile([P, Q], U8, align_bytes=64)
         quantize(nc, g_codes[:], g_scales[:], g_bf[:])
 
-        a_listed = sb.tile([P, I], F32)
-        b = sb.tile([P, I], F32)
+        boost_sb = sb.tile([P, I], F32)
+        nc.scalar.copy(boost_sb[:].rearrange("p (n c) -> p n c", c=4), boost_ps[:].rearrange("p c n -> p n c"))
+        a_listed = sb.tile([P, I], F32, tag="early_values", align_bytes=64)
+        th = sb.tile([P, I], F32)
         for slots, entries in zip(slot_halves, list_halves):
             nc.vector.tensor_copy(a_listed[:, slots], a[:].indirect(offsets[:, entries]))
-            th = sb.tile([P, I // 2], F32, tag="v_bf0", align_bytes=64)
-            nc.scalar.activation(th[:], a_listed[:, slots], ACT.Tanh, scale=neg_half_steep[:])
-            nc.scalar.activation(b[:, slots], th[:], ACT.Copy, scale=-0.5, bias=0.5)
-        boost_sb = sb.tile([P, I], F32)
-        nc.vector.tensor_copy(boost_sb[:].rearrange("p (n c) -> p n c", c=4), boost_ps[:].rearrange("p c n -> p n c"))
-        for slots, entries in zip(slot_halves, list_halves):
-            nc.vector.tensor_tensor(placed[:].indirect(offsets[:, entries]), b[:, slots], boost_sb[:, slots], ALU.mult)
+            nc.scalar.activation(th[:, slots], a_listed[:, slots], ACT.Tanh, scale=neg_half_steep[:])
+        b = sb.tile([P, I], F32)
+        for slots in slot_halves:
+            nc.vector.tensor_scalar(b[:, slots], th[:, slots], -0.5, 0.5, ALU.mult, ALU.add)
+        nc.vector.tensor_tensor(placed[:].indirect(offsets[:]), b[:], boost_sb[:], ALU.mult)
 
-        v_bf = []
-        for c, (lo, hi) in enumerate(VALUE_CHUNKS):
-            grouped = sb.tile([P, hi - lo, PACK], BF16, align_bytes=64, name=f"v_bf{c}", tag=f"v_bf{c}")
-            interleave(nc.scalar.copy, grouped[:], v_raw[c][:])
-            v_bf.append(grouped)
+        v_bf_all = sb.tile([P, PACK * T], BF16, tag="early_values", align_bytes=64)
+        v_bf = [v_bf_all[:, PACK * lo : PACK * hi] for lo, hi in VALUE_CHUNKS]
+        v_bf = [flat.rearrange("p (w j) -> p w j", j=PACK) for flat in v_bf]
+        for c in range(len(VALUE_CHUNKS)):
+            interleave(nc.scalar.copy, v_bf[c], v_raw[c][:])
         fac_ps = ps.tile([P, P], F32, tag="late", bufs=2, name="fac_ps")
         nc.tensor.transpose(fac_ps[:], fac_rows[:], ident[:])
-        after_casts = sb.tile([P, T + T // P], F32, tag=f"v_raw{last}")
+        after_casts = sb.tile([P, 2 * T + BANK + T // P], F32, tag=f"v_raw{last}")
         c0f_t = after_casts[:, 0:T]
-        fac_cols = after_casts[:, T : T + T // P]
+        neg_s = after_casts[:, T : 2 * T]
+        s_second = after_casts[:, 2 * T : 2 * T + BANK]
+        fac_cols = after_casts[:, 2 * T + BANK : 2 * T + BANK + T // P]
         nc.scalar.copy(fac_cols, fac_ps[:, 0 : T // P])
         c0f_ps = [ps.tile([P, BANK], F32, tag="c0f", bufs=2, name="c0f_ps") for cols in token_halves]
         for c, (lo, hi) in enumerate(VALUE_CHUNKS):
             v_codes = sb.tile([P, hi - lo], U32, align_bytes=64, name=f"v_codes{c}")
             v_scales = sb.tile([P, hi - lo], U8, align_bytes=64, name=f"v_scales{c}")
-            quantize(nc, v_codes[:], v_scales[:], v_bf[c][:])
-            c0_t_ps = ps.tile([P, hi - lo], F32, tag="mm", bufs=4, name="c0_t_ps")
+            quantize(nc, v_codes[:], v_scales[:], v_bf[c])
             for t0 in range(lo, hi, P):
+                block = t0 // P
+                c0_t_ps = ps.tile([P, Q], F32, tag=f"bank{block % 4}", name="c0_t_ps")
                 nc.tensor.matmul_mx(
-                    out=c0_t_ps[:, t0 - lo : t0 - lo + P],
+                    out=c0_t_ps[:],
                     lhsT=v_codes[:, t0 - lo : t0 - lo + P].bitcast(FP8X4),
                     lhsT_scale=v_scales[:, t0 - lo : t0 - lo + P],
                     rhs=g_codes[:].bitcast(FP8X4),
@@ -158,27 +162,22 @@ def tile_attend_bboost_heads_kernel(tc, query, keys_words, keys_scales, gout, va
                     start=True,
                     stop=True,
                 )
-            for t0 in range(lo, hi, P):
-                nc.scalar.activation(
-                    c0f_t[:, t0 : t0 + P], c0_t_ps[:, t0 - lo : t0 - lo + P], ACT.Copy, scale=fac_cols[:, t0 // P : t0 // P + 1]
-                )
-            for t0 in range(lo, hi, P):
+                nc.scalar.activation(c0f_t[:, t0 : t0 + P], c0_t_ps[:], ACT.Copy, scale=fac_cols[:, block : block + 1])
                 nc.tensor.transpose(c0f_ps[t0 // BANK][:, t0 % BANK : t0 % BANK + P], c0f_t[:, t0 : t0 + P], ident[:])
 
-        s = sb.tile([P, T], F32, tag="v_bf2", align_bytes=64)
-        nc.vector.tensor_tensor(s[:], a[:], placed[:], ALU.add)
-        after_quant = sb.tile([P, T + I], F32, tag=f"v_bf{last}", align_bytes=64)
-        neg_s = after_quant[:, 0:T]
         first, second = token_halves
+        s_first = sb.tile([P, BANK], F32, tag=f"v_raw{last - 1}")
         neg_max_first = sb.tile([P, 1], F32)
         neg_max = sb.tile([P, 1], F32)
-        nc.vector.tensor_scalar(neg_s[:, first], s[:, first], -1.0, None, ALU.mult, ALU.min, accum_out=neg_max_first[:])
-        nc.vector.tensor_scalar(neg_s[:, second], s[:, second], -1.0, neg_max_first[:], ALU.mult, ALU.min, accum_out=neg_max[:])
+        nc.vector.tensor_tensor(s_first[:], a[:, first], placed[:, first], ALU.add)
+        nc.vector.tensor_scalar(neg_s[:, first], s_first[:], -1.0, None, ALU.mult, ALU.min, accum_out=neg_max_first[:])
+        nc.vector.tensor_tensor(s_second, a[:, second], placed[:, second], ALU.add)
+        nc.vector.tensor_scalar(neg_s[:, second], s_second, -1.0, neg_max_first[:], ALU.mult, ALU.min, accum_out=neg_max[:])
 
-        one_minus_b = after_quant[:, T : T + I]
-        nc.gpsimd.tensor_scalar(one_minus_b, b[:], -1.0, neg_steep_scaled[:], ALU.add, ALU.mult)
+        th_sq = sb.tile([P, I], F32, tag="a")
+        nc.gpsimd.tensor_tensor(th_sq[:], th[:], th[:], ALU.mult)
         sigmoid_slope = sb.tile([P, I], F32)
-        nc.gpsimd.tensor_tensor(sigmoid_slope[:], one_minus_b, b[:], ALU.mult)
+        nc.gpsimd.tensor_scalar(sigmoid_slope[:], th_sq[:], -1.0, neg_steep_scaled[:], ALU.add, ALU.mult)
         slope = sb.tile([P, I], F32)
         nc.gpsimd.tensor_tensor(slope[:], sigmoid_slope[:], boost_sb[:], ALU.mult)
 
@@ -189,21 +188,21 @@ def tile_attend_bboost_heads_kernel(tc, query, keys_words, keys_scales, gout, va
         nc.scalar.activation(p[:, first], neg_s[:, first], ACT.Exp, bias=neg_max_first[:], scale=-1.0, accum_out=z_first[:])
         nc.scalar.activation(shift[:], neg_max_first[:], ACT.Exp, bias=neg_max[:], scale=-1.0)
         nc.scalar.activation(p[:, second], neg_s[:, second], ACT.Exp, bias=neg_max[:], scale=-1.0, accum_out=z_second[:])
-        z = sb.tile([P, 1], F32, tag="z")
+        z = sb.tile([P, 1], F32)
         nc.scalar.activation(z[:], z_first[:], ACT.Identity, bias=z_second[:], scale=shift[:])
 
         u_first = sb.tile([P, BANK], F32)
         sum_first = sb.tile([P, 1], F32)
         nc.vector.scalar_tensor_tensor(u_first[:], c0f_ps[0][:], 1.0, p[:, first], ALU.mult, ALU.mult, accum_out=sum_first[:])
         sum_first_shifted = sb.tile([P, 1], F32)
-        nc.vector.tensor_tensor(sum_first_shifted[:], sum_first[:], shift[:], ALU.mult)
-        rz = sb.tile([P, 1], F32)
-        nc.vector.reciprocal(rz[:], z[:])
-        u_second = sb.tile([P, BANK], F32, tag="z")
+        nc.vector.tensor_scalar(sum_first_shifted[:], sum_first[:], shift[:], None, ALU.mult)
+        u_second = sb.tile([P, BANK], F32)
         sum_second = sb.tile([P, 1], F32)
         nc.vector.scalar_tensor_tensor(u_second[:], c0f_ps[1][:], 1.0, p[:, second], ALU.mult, ALU.mult, accum_out=sum_second[:])
+        rz = sb.tile([P, 1], F32)
+        nc.vector.reciprocal(rz[:], z[:])
         rz_first = sb.tile([P, 1], F32)
-        nc.vector.tensor_tensor(rz_first[:], rz[:], shift[:], ALU.mult)
+        nc.vector.tensor_scalar(rz_first[:], rz[:], shift[:], None, ALU.mult)
         mean = sb.tile([P, 1], F32)
         nc.vector.tensor_scalar(mean[:], sum_first_shifted[:], sum_second[:], rz[:], ALU.add, ALU.mult)
         pn = sb.tile([P, T], F32)
@@ -217,7 +216,7 @@ def tile_attend_bboost_heads_kernel(tc, query, keys_words, keys_scales, gout, va
         nc.vector.tensor_copy(ds_listed[:], ds[:].indirect(offsets[:]))
         nc.vector.tensor_tensor(placed[:].indirect(offsets[:]), ds_listed[:], slope[:], ALU.mult)
 
-        sum_ps = [ps.tile([P, BANK], F32, tag="mm", bufs=4, name="sum_ps") for cols in token_halves]
+        sum_ps = [ps.tile([P, BANK], F32, tag=f"bank{2 + h}", name="sum_ps") for h in range(2)]
         for t0 in range(0, T, P):
             at = t0 % BANK
             nc.tensor.matmul(

@@ -62,20 +62,24 @@ def tile_attend_bboost_heads_kernel(tc, query, keys_words, keys_scales, gout, va
                 out=k_scales[32 * quad : 32 * quad + 4, :].bitcast(I32),
                 in_=keys_scales[0, 4 * quad : 4 * quad + 4, :].bitcast(I32),
             )
-        g_raw = sb.tile([P, PACK, Q], F32)
-        nc.sync.dma_start(out=g_raw[:], in_=gout.rearrange("(p j) w -> p j w", j=PACK))
+        vals_pj = vals.rearrange("(p j) w -> p j w", j=PACK)
+        v_raw = [sb.tile([P, PACK, hi - lo], F32, name=f"v_raw{c}", tag=f"v_raw{c}") for c, (lo, hi) in enumerate(VALUE_CHUNKS)]
+
+        def load_values(c):
+            lo, hi = VALUE_CHUNKS[c]
+            nc.sync.dma_start(out=v_raw[c][:], in_=vals_pj[:, :, lo:hi])
+
+        load_values(0)
         offsets = sb.tile([P, I // 16], U16)
         nc.sync.dma_start(offsets[:], offs)
         steep_sb = sb.tile([P, 1], F32)
         nc.sync.dma_start(out=steep_sb[:], in_=steep)
-        vals_pj = vals.rearrange("(p j) w -> p j w", j=PACK)
-        v_raw = []
-        for c, (lo, hi) in enumerate(VALUE_CHUNKS):
-            raw = sb.tile([P, PACK, hi - lo], F32, name=f"v_raw{c}", tag=f"v_raw{c}")
-            nc.sync.dma_start(out=raw[:], in_=vals_pj[:, :, lo:hi])
-            v_raw.append(raw)
-            if c == 1:
-                nc.sync.dma_start(out=fac_rows[0 : T // P, :], in_=fac.rearrange("o (c n) -> (o c) n", n=P))
+        g_raw = sb.tile([P, PACK, Q], F32)
+        nc.sync.dma_start(out=g_raw[:], in_=gout.rearrange("(p j) w -> p j w", j=PACK))
+        load_values(1)
+        nc.sync.dma_start(out=fac_rows[0 : T // P, :], in_=fac.rearrange("o (c n) -> (o c) n", n=P))
+        for c in range(2, len(VALUE_CHUNKS)):
+            load_values(c)
         old_sb = sb.tile([P, T], F32)
         nc.sync.dma_start(out=old_sb[:], in_=old)
         ident = sb.tile([P, P], F32)
@@ -114,29 +118,34 @@ def tile_attend_bboost_heads_kernel(tc, query, keys_words, keys_scales, gout, va
         for c in range(4):
             nc.tensor.transpose(boost_ps[:, c, :], boost_held[:, c : c + 1].to_broadcast([P, P]), ident[:])
 
-        g_bf = sb.tile([P, Q, PACK], BF16, align_bytes=64)
+        v_codes = sb.tile([P, T], U32, align_bytes=64)
+        v_scales = sb.tile([P, T], U8, align_bytes=64)
+        first_width = VALUE_CHUNKS[0][1]
+        v_bf_first = sb.tile([P, first_width, PACK], BF16, align_bytes=64)
+        interleave(nc.vector.tensor_copy, v_bf_first[:], v_raw[0][:])
+        quantize(nc, v_codes[:, 0:first_width], v_scales[:, 0:first_width], v_bf_first[:])
+
+        boost_sb = sb.tile([P, I], F32)
+        nc.scalar.copy(boost_sb[:].rearrange("p (n c) -> p n c", c=4), boost_ps[:].rearrange("p c n -> p n c"))
+        th = sb.tile([P, I], F32)
+        b = sb.tile([P, I], F32)
+        for h, (slots, entries) in enumerate(zip(slot_halves, list_halves)):
+            a_listed = sb.tile([P, I // 2], F32, tag=f"a_listed{h}", align_bytes=64)
+            nc.vector.tensor_copy(a_listed[:], a[:].indirect(offsets[:, entries]))
+            nc.scalar.activation(th[:, slots], a_listed[:], ACT.Tanh, scale=neg_half_steep[:])
+            nc.vector.tensor_scalar(b[:, slots], th[:, slots], -0.5, 0.5, ALU.mult, ALU.add)
+        g_bf = sb.tile([P, Q, PACK], BF16, tag="a_listed0", align_bytes=64)
         interleave(nc.vector.tensor_copy, g_bf[:], g_raw[:])
         g_codes = sb.tile([P, Q], U32, align_bytes=64)
         g_scales = sb.tile([P, Q], U8, align_bytes=64)
         quantize(nc, g_codes[:], g_scales[:], g_bf[:])
-
-        boost_sb = sb.tile([P, I], F32)
-        nc.scalar.copy(boost_sb[:].rearrange("p (n c) -> p n c", c=4), boost_ps[:].rearrange("p c n -> p n c"))
-        a_listed = sb.tile([P, I], F32, tag="early_values", align_bytes=64)
-        th = sb.tile([P, I], F32)
-        for slots, entries in zip(slot_halves, list_halves):
-            nc.vector.tensor_copy(a_listed[:, slots], a[:].indirect(offsets[:, entries]))
-            nc.scalar.activation(th[:, slots], a_listed[:, slots], ACT.Tanh, scale=neg_half_steep[:])
-        b = sb.tile([P, I], F32)
-        for slots in slot_halves:
-            nc.vector.tensor_scalar(b[:, slots], th[:, slots], -0.5, 0.5, ALU.mult, ALU.add)
         nc.vector.tensor_tensor(placed[:].indirect(offsets[:]), b[:], boost_sb[:], ALU.mult)
 
-        v_bf_all = sb.tile([P, PACK * T], BF16, tag="early_values", align_bytes=64)
-        v_bf = [v_bf_all[:, PACK * lo : PACK * hi] for lo, hi in VALUE_CHUNKS]
-        v_bf = [flat.rearrange("p (w j) -> p w j", j=PACK) for flat in v_bf]
-        for c in range(len(VALUE_CHUNKS)):
-            interleave(nc.scalar.copy, v_bf[c], v_raw[c][:])
+        v_bf_rest = sb.tile([P, PACK * (T - first_width)], BF16, tag="a_listed1", align_bytes=64)
+        for c, (lo, hi) in list(enumerate(VALUE_CHUNKS))[1:]:
+            grouped = v_bf_rest[:, PACK * (lo - first_width) : PACK * (hi - first_width)].rearrange("p (w j) -> p w j", j=PACK)
+            interleave(nc.scalar.copy, grouped, v_raw[c][:])
+            quantize(nc, v_codes[:, lo:hi], v_scales[:, lo:hi], grouped)
         fac_ps = ps.tile([P, P], F32, tag="late", bufs=2, name="fac_ps")
         nc.tensor.transpose(fac_ps[:], fac_rows[:], ident[:])
         after_casts = sb.tile([P, 2 * T + BANK + T // P], F32, tag=f"v_raw{last}")
@@ -146,24 +155,20 @@ def tile_attend_bboost_heads_kernel(tc, query, keys_words, keys_scales, gout, va
         fac_cols = after_casts[:, 2 * T + BANK : 2 * T + BANK + T // P]
         nc.scalar.copy(fac_cols, fac_ps[:, 0 : T // P])
         c0f_ps = [ps.tile([P, BANK], F32, tag="c0f", bufs=2, name="c0f_ps") for cols in token_halves]
-        for c, (lo, hi) in enumerate(VALUE_CHUNKS):
-            v_codes = sb.tile([P, hi - lo], U32, align_bytes=64, name=f"v_codes{c}")
-            v_scales = sb.tile([P, hi - lo], U8, align_bytes=64, name=f"v_scales{c}")
-            quantize(nc, v_codes[:], v_scales[:], v_bf[c])
-            for t0 in range(lo, hi, P):
-                block = t0 // P
-                c0_t_ps = ps.tile([P, Q], F32, tag=f"bank{block % 4}", name="c0_t_ps")
-                nc.tensor.matmul_mx(
-                    out=c0_t_ps[:],
-                    lhsT=v_codes[:, t0 - lo : t0 - lo + P].bitcast(FP8X4),
-                    lhsT_scale=v_scales[:, t0 - lo : t0 - lo + P],
-                    rhs=g_codes[:].bitcast(FP8X4),
-                    rhs_scale=g_scales[:],
-                    start=True,
-                    stop=True,
-                )
-                nc.scalar.activation(c0f_t[:, t0 : t0 + P], c0_t_ps[:], ACT.Copy, scale=fac_cols[:, block : block + 1])
-                nc.tensor.transpose(c0f_ps[t0 // BANK][:, t0 % BANK : t0 % BANK + P], c0f_t[:, t0 : t0 + P], ident[:])
+        for t0 in range(0, T, P):
+            block = t0 // P
+            c0_t_ps = ps.tile([P, Q], F32, tag=f"bank{block % 4}", name="c0_t_ps")
+            nc.tensor.matmul_mx(
+                out=c0_t_ps[:],
+                lhsT=v_codes[:, t0 : t0 + P].bitcast(FP8X4),
+                lhsT_scale=v_scales[:, t0 : t0 + P],
+                rhs=g_codes[:].bitcast(FP8X4),
+                rhs_scale=g_scales[:],
+                start=True,
+                stop=True,
+            )
+            nc.scalar.activation(c0f_t[:, t0 : t0 + P], c0_t_ps[:], ACT.Copy, scale=fac_cols[:, block : block + 1])
+            nc.tensor.transpose(c0f_ps[t0 // BANK][:, t0 % BANK : t0 % BANK + P], c0f_t[:, t0 : t0 + P], ident[:])
 
         first, second = token_halves
         s_first = sb.tile([P, BANK], F32, tag=f"v_raw{last - 1}")
@@ -183,28 +188,34 @@ def tile_attend_bboost_heads_kernel(tc, query, keys_words, keys_scales, gout, va
 
         p = sb.tile([P, T], F32)
         z_first = sb.tile([P, 1], F32)
-        z_second = sb.tile([P, 1], F32)
+        z_second = sb.tile([P, 1], F32, tag="z_second")
         shift = sb.tile([P, 1], F32)
         nc.scalar.activation(p[:, first], neg_s[:, first], ACT.Exp, bias=neg_max_first[:], scale=-1.0, accum_out=z_first[:])
-        nc.scalar.activation(shift[:], neg_max_first[:], ACT.Exp, bias=neg_max[:], scale=-1.0)
         nc.scalar.activation(p[:, second], neg_s[:, second], ACT.Exp, bias=neg_max[:], scale=-1.0, accum_out=z_second[:])
+        nc.scalar.activation(shift[:], neg_max_first[:], ACT.Exp, bias=neg_max[:], scale=-1.0)
         z = sb.tile([P, 1], F32)
         nc.scalar.activation(z[:], z_first[:], ACT.Identity, bias=z_second[:], scale=shift[:])
 
-        u_first = sb.tile([P, BANK], F32)
-        sum_first = sb.tile([P, 1], F32)
-        nc.vector.scalar_tensor_tensor(u_first[:], c0f_ps[0][:], 1.0, p[:, first], ALU.mult, ALU.mult, accum_out=sum_first[:])
-        sum_first_shifted = sb.tile([P, 1], F32)
-        nc.vector.tensor_scalar(sum_first_shifted[:], sum_first[:], shift[:], None, ALU.mult)
-        u_second = sb.tile([P, BANK], F32)
-        sum_second = sb.tile([P, 1], F32)
-        nc.vector.scalar_tensor_tensor(u_second[:], c0f_ps[1][:], 1.0, p[:, second], ALU.mult, ALU.mult, accum_out=sum_second[:])
+        def weighted_sum(lo, hi, tag):
+            products = sb.tile([P, hi - lo], F32, tag=tag, name="products")
+            total = sb.tile([P, 1], F32, name=f"total{lo}")
+            nc.vector.scalar_tensor_tensor(
+                products[:], c0f_ps[lo // BANK][:, lo % BANK : lo % BANK + hi - lo], 1.0, p[:, lo:hi], ALU.mult, ALU.mult, accum_out=total[:]
+            )
+            return total
+
+        quarter = T // 4
+        sum_first = weighted_sum(0, BANK, "products_first")
+        sum_third = weighted_sum(BANK, BANK + quarter, "products_third")
         rz = sb.tile([P, 1], F32)
         nc.vector.reciprocal(rz[:], z[:])
+        sum_fourth = weighted_sum(BANK + quarter, T, "z_second")
+        sum_three = sb.tile([P, 1], F32)
+        nc.vector.tensor_scalar(sum_three[:], sum_first[:], shift[:], sum_third[:], ALU.mult, ALU.add)
         rz_first = sb.tile([P, 1], F32)
         nc.vector.tensor_scalar(rz_first[:], rz[:], shift[:], None, ALU.mult)
         mean = sb.tile([P, 1], F32)
-        nc.vector.tensor_scalar(mean[:], sum_first_shifted[:], sum_second[:], rz[:], ALU.add, ALU.mult)
+        nc.vector.tensor_scalar(mean[:], sum_three[:], sum_fourth[:], rz[:], ALU.add, ALU.mult)
         pn = sb.tile([P, T], F32)
         ds = sb.tile([P, T], F32)
         for h, norm in ((1, rz), (0, rz_first)):
@@ -240,5 +251,10 @@ def tile_attend_bboost_heads_kernel(tc, query, keys_words, keys_scales, gout, va
                 nc.tensor.transpose(dense_ps[:, at : at + P], dense_t[:, t0 : t0 + P], ident[:])
             for at in range(0, BANK, OUT_PIECE):
                 piece = slice(h * BANK + at, h * BANK + at + OUT_PIECE)
-                nc.vector.tensor_tensor(res[:, piece], dense_ps[:, at : at + OUT_PIECE], placed[:, piece], ALU.add)
+                if piece.start == BANK:
+                    dense_piece = sb.tile([P, OUT_PIECE], F32)
+                    nc.scalar.copy(dense_piece[:], dense_ps[:, at : at + OUT_PIECE])
+                    nc.gpsimd.tensor_tensor(res[:, piece], dense_piece[:], placed[:, piece], ALU.add)
+                else:
+                    nc.vector.tensor_tensor(res[:, piece], dense_ps[:, at : at + OUT_PIECE], placed[:, piece], ALU.add)
                 nc.sync.dma_start(out=out[:, piece], in_=res[:, piece])

@@ -20,10 +20,11 @@ ALU = mybir.AluOpType
 P = 128
 PACK = 4
 BANK = 512
+ENTRIES_PER_COLUMN = 16
 OUT_SCALE = 1024.0
-SCORE_PIECES = ((0, 256), (256, 512), (512, 768), (768, 1024))
-VALUE_CHUNKS = ((0, 256), (256, 512), (512, 768), (768, 1024))
-OUT_PIECE = 256
+QUARTER = T // 4
+QUARTERS = tuple((lo, lo + QUARTER) for lo in range(0, T, QUARTER))
+BOOST_PER_PARTITION = I // P
 
 
 def interleave(copy, grouped, raw):
@@ -36,10 +37,10 @@ def quantize(nc, codes, scales, grouped):
 
 def tile_attend_bboost_heads_kernel(tc, query, keys_words, keys_scales, gout, vals, steep, boost, fac, old, offs, out):
     nc = tc.nc
-    last = len(VALUE_CHUNKS) - 1
+    last = len(QUARTERS) - 1
     token_halves = [slice(0, BANK), slice(BANK, T)]
     slot_halves = [slice(0, I // 2), slice(I // 2, I)]
-    list_halves = [slice(0, I // 32), slice(I // 32, I // 16)]
+    list_halves = [slice(s.start // ENTRIES_PER_COLUMN, s.stop // ENTRIES_PER_COLUMN) for s in slot_halves]
     with ExitStack() as ctx:
         sb = ctx.enter_context(tc.tile_pool(name="sb", bufs=1))
         ps = ctx.enter_context(tc.psum_pool(name="ps", bufs=1))
@@ -53,8 +54,8 @@ def tile_attend_bboost_heads_kernel(tc, query, keys_words, keys_scales, gout, va
 
         q_raw = sb.tile([P, PACK, Q], F32)
         nc.sync.dma_start(out=q_raw[:], in_=query.rearrange("(p j) w -> p j w", j=PACK))
-        boost_cols = sb.tile([P, 4], F32)
-        nc.sync.dma_start(out=boost_cols[:], in_=boost.rearrange("o (p c) -> (o p) c", c=4))
+        boost_cols = sb.tile([P, BOOST_PER_PARTITION], F32)
+        nc.sync.dma_start(out=boost_cols[:], in_=boost.rearrange("o (p c) -> (o p) c", c=BOOST_PER_PARTITION))
         k_words = sb.tile([P, 2 * T], U8, align_bytes=64)
         nc.sync.dma_start(out=k_words[:].bitcast(I32), in_=keys_words[0].bitcast(I32))
         for quad in range(4):
@@ -63,14 +64,14 @@ def tile_attend_bboost_heads_kernel(tc, query, keys_words, keys_scales, gout, va
                 in_=keys_scales[0, 4 * quad : 4 * quad + 4, :].bitcast(I32),
             )
         vals_pj = vals.rearrange("(p j) w -> p j w", j=PACK)
-        v_raw = [sb.tile([P, PACK, hi - lo], F32, name=f"v_raw{c}", tag=f"v_raw{c}") for c, (lo, hi) in enumerate(VALUE_CHUNKS)]
+        v_raw = [sb.tile([P, PACK, hi - lo], F32, name=f"v_raw{c}", tag=f"v_raw{c}") for c, (lo, hi) in enumerate(QUARTERS)]
 
         def load_values(c):
-            lo, hi = VALUE_CHUNKS[c]
+            lo, hi = QUARTERS[c]
             nc.sync.dma_start(out=v_raw[c][:], in_=vals_pj[:, :, lo:hi])
 
         load_values(0)
-        offsets = sb.tile([P, I // 16], U16)
+        offsets = sb.tile([P, I // ENTRIES_PER_COLUMN], U16)
         nc.sync.dma_start(offsets[:], offs)
         steep_sb = sb.tile([P, 1], F32)
         nc.sync.dma_start(out=steep_sb[:], in_=steep)
@@ -78,7 +79,7 @@ def tile_attend_bboost_heads_kernel(tc, query, keys_words, keys_scales, gout, va
         nc.sync.dma_start(out=g_raw[:], in_=gout.rearrange("(p j) w -> p j w", j=PACK))
         load_values(1)
         nc.sync.dma_start(out=fac_rows[0 : T // P, :], in_=fac.rearrange("o (c n) -> (o c) n", n=P))
-        for c in range(2, len(VALUE_CHUNKS)):
+        for c in range(2, len(QUARTERS)):
             load_values(c)
         old_sb = sb.tile([P, T], F32)
         nc.sync.dma_start(out=old_sb[:], in_=old)
@@ -99,7 +100,7 @@ def tile_attend_bboost_heads_kernel(tc, query, keys_words, keys_scales, gout, va
         for cols in q_halves:
             quantize(nc, q_codes[:, cols], q_scales[:, cols], q_bf[:, cols, :])
         a = sb.tile([P, T], F32, tag="a")
-        for c, (lo, hi) in enumerate(SCORE_PIECES):
+        for c, (lo, hi) in enumerate(QUARTERS):
             a_ps = ps.tile([P, hi - lo], F32, tag=f"bank{c}", name="a_ps")
             nc.tensor.matmul_mx(
                 out=a_ps[:],
@@ -112,21 +113,22 @@ def tile_attend_bboost_heads_kernel(tc, query, keys_words, keys_scales, gout, va
             )
             nc.scalar.copy(a[:, lo:hi], a_ps[:])
 
-        boost_held = sb.tile([P, 4], F32, tag="q_bf", align_bytes=64)
+        boost_held = sb.tile([P, BOOST_PER_PARTITION], F32, tag="q_bf", align_bytes=64)
         nc.vector.tensor_copy(boost_held[:], boost_cols[:])
-        boost_ps = ps.tile([P, 4, P], F32, tag="late", bufs=2, name="boost_ps")
-        for c in range(4):
+        boost_ps = ps.tile([P, BOOST_PER_PARTITION, P], F32, tag="spread", bufs=2, name="boost_ps")
+        for c in range(BOOST_PER_PARTITION):
             nc.tensor.transpose(boost_ps[:, c, :], boost_held[:, c : c + 1].to_broadcast([P, P]), ident[:])
 
         v_codes = sb.tile([P, T], U32, align_bytes=64)
         v_scales = sb.tile([P, T], U8, align_bytes=64)
-        first_width = VALUE_CHUNKS[0][1]
-        v_bf_first = sb.tile([P, first_width, PACK], BF16, align_bytes=64)
+        v_bf_first = sb.tile([P, QUARTER, PACK], BF16, align_bytes=64)
         interleave(nc.vector.tensor_copy, v_bf_first[:], v_raw[0][:])
-        quantize(nc, v_codes[:, 0:first_width], v_scales[:, 0:first_width], v_bf_first[:])
+        quantize(nc, v_codes[:, 0:QUARTER], v_scales[:, 0:QUARTER], v_bf_first[:])
 
         boost_sb = sb.tile([P, I], F32)
-        nc.scalar.copy(boost_sb[:].rearrange("p (n c) -> p n c", c=4), boost_ps[:].rearrange("p c n -> p n c"))
+        nc.scalar.copy(
+            boost_sb[:].rearrange("p (n c) -> p n c", c=BOOST_PER_PARTITION), boost_ps[:].rearrange("p c n -> p n c")
+        )
         th = sb.tile([P, I], F32)
         b = sb.tile([P, I], F32)
         for h, (slots, entries) in enumerate(zip(slot_halves, list_halves)):
@@ -141,23 +143,24 @@ def tile_attend_bboost_heads_kernel(tc, query, keys_words, keys_scales, gout, va
         quantize(nc, g_codes[:], g_scales[:], g_bf[:])
         nc.vector.tensor_tensor(placed[:].indirect(offsets[:]), b[:], boost_sb[:], ALU.mult)
 
-        v_bf_rest = sb.tile([P, PACK * (T - first_width)], BF16, tag="a_listed1", align_bytes=64)
-        for c, (lo, hi) in list(enumerate(VALUE_CHUNKS))[1:]:
-            grouped = v_bf_rest[:, PACK * (lo - first_width) : PACK * (hi - first_width)].rearrange("p (w j) -> p w j", j=PACK)
+        v_bf_rest = sb.tile([P, PACK * (T - QUARTER)], BF16, tag="a_listed1", align_bytes=64)
+        for c, (lo, hi) in list(enumerate(QUARTERS))[1:]:
+            grouped = v_bf_rest[:, PACK * (lo - QUARTER) : PACK * (hi - QUARTER)].rearrange("p (w j) -> p w j", j=PACK)
             interleave(nc.scalar.copy, grouped, v_raw[c][:])
             quantize(nc, v_codes[:, lo:hi], v_scales[:, lo:hi], grouped)
-        fac_ps = ps.tile([P, P], F32, tag="late", bufs=2, name="fac_ps")
+
+        fac_ps = ps.tile([P, P], F32, tag="spread", bufs=2, name="fac_ps")
         nc.tensor.transpose(fac_ps[:], fac_rows[:], ident[:])
-        after_casts = sb.tile([P, 2 * T + BANK + T // P], F32, tag=f"v_raw{last}")
-        c0f_t = after_casts[:, 0:T]
-        neg_s = after_casts[:, T : 2 * T]
-        s_second = after_casts[:, 2 * T : 2 * T + BANK]
-        fac_cols = after_casts[:, 2 * T + BANK : 2 * T + BANK + T // P]
+        after_rounding = sb.tile([P, 2 * T + BANK + T // P], F32, tag=f"v_raw{last}")
+        c0f_t = after_rounding[:, 0:T]
+        neg_s = after_rounding[:, T : 2 * T]
+        s_second = after_rounding[:, 2 * T : 2 * T + BANK]
+        fac_cols = after_rounding[:, 2 * T + BANK : 2 * T + BANK + T // P]
         nc.scalar.copy(fac_cols, fac_ps[:, 0 : T // P])
         c0f_ps = [ps.tile([P, BANK], F32, tag="c0f", bufs=2, name="c0f_ps") for cols in token_halves]
         for t0 in range(0, T, P):
             block = t0 // P
-            c0_t_ps = ps.tile([P, Q], F32, tag=f"bank{block % 4}", name="c0_t_ps")
+            c0_t_ps = ps.tile([P, Q], F32, tag=f"bank{block % len(QUARTERS)}", name="c0_t_ps")
             nc.tensor.matmul_mx(
                 out=c0_t_ps[:],
                 lhsT=v_codes[:, t0 : t0 + P].bitcast(FP8X4),
@@ -199,23 +202,22 @@ def tile_attend_bboost_heads_kernel(tc, query, keys_words, keys_scales, gout, va
         def weighted_sum(lo, hi, tag):
             products = sb.tile([P, hi - lo], F32, tag=tag, name="products")
             total = sb.tile([P, 1], F32, name=f"total{lo}")
-            nc.vector.scalar_tensor_tensor(
-                products[:], c0f_ps[lo // BANK][:, lo % BANK : lo % BANK + hi - lo], 1.0, p[:, lo:hi], ALU.mult, ALU.mult, accum_out=total[:]
-            )
+            c0f = c0f_ps[lo // BANK][:, lo % BANK : lo % BANK + hi - lo]
+            nc.vector.scalar_tensor_tensor(products[:], c0f, 1.0, p[:, lo:hi], ALU.mult, ALU.mult, accum_out=total[:])
             return total
 
-        quarter = T // 4
         sum_first = weighted_sum(0, BANK, "products_first")
-        sum_third = weighted_sum(BANK, BANK + quarter, "products_third")
+        sum_third = weighted_sum(BANK, BANK + QUARTER, "products_third")
         rz = sb.tile([P, 1], F32)
         nc.vector.reciprocal(rz[:], z[:])
-        sum_fourth = weighted_sum(BANK + quarter, T, "z_second")
+        sum_fourth = weighted_sum(BANK + QUARTER, T, "z_second")
         sum_three = sb.tile([P, 1], F32)
         nc.vector.tensor_scalar(sum_three[:], sum_first[:], shift[:], sum_third[:], ALU.mult, ALU.add)
         rz_first = sb.tile([P, 1], F32)
         nc.vector.tensor_scalar(rz_first[:], rz[:], shift[:], None, ALU.mult)
         mean = sb.tile([P, 1], F32)
         nc.vector.tensor_scalar(mean[:], sum_three[:], sum_fourth[:], rz[:], ALU.add, ALU.mult)
+
         pn = sb.tile([P, T], F32)
         ds = sb.tile([P, T], F32)
         for h, norm in ((1, rz), (0, rz_first)):
@@ -245,16 +247,18 @@ def tile_attend_bboost_heads_kernel(tc, query, keys_words, keys_scales, gout, va
                     sum_ps[h][:, at : at + P], ds_scaled[:, t0 : t0 + P], ident[:], start=False, stop=at == BANK - P, is_transpose=True
                 )
             nc.scalar.copy(dense_t[:, cols], sum_ps[h][:])
-            dense_ps = ps.tile([P, BANK], F32, tag="late", bufs=2, name="dense_ps")
+            dense_ps = ps.tile([P, BANK], F32, tag="spread", bufs=2, name="dense_ps")
             for at in range(0, BANK, P):
                 t0 = h * BANK + at
                 nc.tensor.transpose(dense_ps[:, at : at + P], dense_t[:, t0 : t0 + P], ident[:])
-            for at in range(0, BANK, OUT_PIECE):
-                piece = slice(h * BANK + at, h * BANK + at + OUT_PIECE)
+
+            for at in range(0, BANK, QUARTER):
+                piece = slice(h * BANK + at, h * BANK + at + QUARTER)
                 if piece.start == BANK:
-                    dense_piece = sb.tile([P, OUT_PIECE], F32)
-                    nc.scalar.copy(dense_piece[:], dense_ps[:, at : at + OUT_PIECE])
+                    dense_piece = sb.tile([P, QUARTER], F32)
+                    nc.scalar.copy(dense_piece[:], dense_ps[:, at : at + QUARTER])
                     nc.gpsimd.tensor_tensor(res[:, piece], dense_piece[:], placed[:, piece], ALU.add)
+                    nc.scalar.dma_start(out=out[:, piece], in_=res[:, piece])
                 else:
-                    nc.vector.tensor_tensor(res[:, piece], dense_ps[:, at : at + OUT_PIECE], placed[:, piece], ALU.add)
-                nc.sync.dma_start(out=out[:, piece], in_=res[:, piece])
+                    nc.vector.tensor_tensor(res[:, piece], dense_ps[:, at : at + QUARTER], placed[:, piece], ALU.add)
+                    nc.sync.dma_start(out=out[:, piece], in_=res[:, piece])

from contextlib import ExitStack

import concourse.mybir as mybir
from concourse.masks import make_identity

D, E, T, Q, I = 512, 512, 1024, 128, 512
FLOPS = 2 * Q * T * (D + E)

F32 = mybir.dt.float32
BF16 = mybir.dt.bfloat16
I32 = mybir.dt.int32
U32 = mybir.dt.uint32
U16 = mybir.dt.uint16
U8 = mybir.dt.uint8
FP8X4 = mybir.dt.float8_e4m3fn_x4
FP4X4 = mybir.dt.float4_e2m1fn_x4
ACT = mybir.ActivationFunctionType
ALU = mybir.AluOpType

P = 128
PACK = 4
BANK = 512
ENTRIES_PER_COLUMN = 16
OUT_SCALE = 1024.0
QUARTER = T // 4
QUARTERS = tuple((lo, lo + QUARTER) for lo in range(0, T, QUARTER))
BOOST_PER_PARTITION = I // P


def interleave(copy, grouped, raw):
    copy(grouped.rearrange("p (c i) t -> p c t i", i=4), raw.rearrange("p t (c i) -> p c t i", i=4))


def quantize(nc, codes, scales, grouped):
    nc.vector.quantize_mx(out=codes.bitcast(FP8X4), scales=scales, in_=grouped.rearrange("p w j -> p (w j)"))


def tile_attend_bboost_heads_kernel(tc, query, keys_words, keys_scales, gout, vals, steep, boost, fac, old, offs, out):
    nc = tc.nc
    last = len(QUARTERS) - 1
    token_halves = [slice(0, BANK), slice(BANK, T)]
    slot_halves = [slice(0, I // 2), slice(I // 2, I)]
    list_halves = [slice(s.start // ENTRIES_PER_COLUMN, s.stop // ENTRIES_PER_COLUMN) for s in slot_halves]
    with ExitStack() as ctx:
        sb = ctx.enter_context(tc.tile_pool(name="sb", bufs=1))
        ps = ctx.enter_context(tc.psum_pool(name="ps", bufs=1))

        k_scales = sb.tile([P, T], U8, align_bytes=64)
        nc.gpsimd.memset(k_scales[:].bitcast(I32), 0)
        fac_rows = sb.tile([P, P], F32)
        nc.vector.memset(fac_rows[:], 0.0)
        placed = sb.tile([P, T], F32)
        nc.vector.memset(placed[:], 0.0)

        q_raw = sb.tile([P, PACK, Q], F32)
        nc.sync.dma_start(out=q_raw[:], in_=query.rearrange("(p j) w -> p j w", j=PACK))
        boost_cols = sb.tile([P, BOOST_PER_PARTITION], F32)
        nc.sync.dma_start(out=boost_cols[:], in_=boost.rearrange("o (p c) -> (o p) c", c=BOOST_PER_PARTITION))
        k_words = sb.tile([P, 2 * T], U8, align_bytes=64)
        nc.sync.dma_start(out=k_words[:].bitcast(I32), in_=keys_words[0].bitcast(I32))
        for quad in range(4):
            nc.sync.dma_start(
                out=k_scales[32 * quad : 32 * quad + 4, :].bitcast(I32),
                in_=keys_scales[0, 4 * quad : 4 * quad + 4, :].bitcast(I32),
            )
        vals_pj = vals.rearrange("(p j) w -> p j w", j=PACK)
        v_raw = [sb.tile([P, PACK, hi - lo], F32, name=f"v_raw{c}", tag=f"v_raw{c}") for c, (lo, hi) in enumerate(QUARTERS)]

        def load_values(c):
            lo, hi = QUARTERS[c]
            nc.sync.dma_start(out=v_raw[c][:], in_=vals_pj[:, :, lo:hi])

        load_values(0)
        offsets = sb.tile([P, I // ENTRIES_PER_COLUMN], U16)
        nc.sync.dma_start(offsets[:], offs)
        steep_sb = sb.tile([P, 1], F32)
        nc.sync.dma_start(out=steep_sb[:], in_=steep)
        g_raw = sb.tile([P, PACK, Q], F32)
        nc.sync.dma_start(out=g_raw[:], in_=gout.rearrange("(p j) w -> p j w", j=PACK))
        load_values(1)
        nc.sync.dma_start(out=fac_rows[0 : T // P, :], in_=fac.rearrange("o (c n) -> (o c) n", n=P))
        for c in range(2, len(QUARTERS)):
            load_values(c)
        old_sb = sb.tile([P, T], F32)
        nc.sync.dma_start(out=old_sb[:], in_=old)
        ident = sb.tile([P, P], F32)
        make_identity(nc, ident[:])

        neg_half_steep = sb.tile([P, 1], F32)
        nc.gpsimd.tensor_scalar(neg_half_steep[:], steep_sb[:], -0.5, 0.0, ALU.mult, ALU.add)
        neg_steep_scaled = sb.tile([P, 1], F32)
        nc.gpsimd.tensor_scalar(neg_steep_scaled[:], steep_sb[:], -0.25 * OUT_SCALE, 0.0, ALU.mult, ALU.add)

        q_bf = sb.tile([P, Q, PACK], BF16, tag="q_bf", align_bytes=64)
        q_codes = sb.tile([P, Q], U32, align_bytes=64)
        q_scales = sb.tile([P, Q], U8, align_bytes=64)
        q_halves = [slice(0, Q // 2), slice(Q // 2, Q)]
        for cols in q_halves:
            interleave(nc.vector.tensor_copy, q_bf[:, cols, :], q_raw[:, :, cols])
        for cols in q_halves:
            quantize(nc, q_codes[:, cols], q_scales[:, cols], q_bf[:, cols, :])
        a = sb.tile([P, T], F32, tag="a")
        for c, (lo, hi) in enumerate(QUARTERS):
            a_ps = ps.tile([P, hi - lo], F32, tag=f"bank{c}", name="a_ps")
            nc.tensor.matmul_mx(
                out=a_ps[:],
                lhsT=q_codes[:].bitcast(FP8X4),
                lhsT_scale=q_scales[:],
                rhs=k_words[:, 2 * lo : 2 * hi].bitcast(FP4X4),
                rhs_scale=k_scales[:, lo:hi],
                start=True,
                stop=True,
            )
            nc.scalar.copy(a[:, lo:hi], a_ps[:])

        boost_held = sb.tile([P, BOOST_PER_PARTITION], F32, tag="q_bf", align_bytes=64)
        nc.vector.tensor_copy(boost_held[:], boost_cols[:])
        boost_ps = ps.tile([P, BOOST_PER_PARTITION, P], F32, tag="spread", bufs=2, name="boost_ps")
        for c in range(BOOST_PER_PARTITION):
            nc.tensor.transpose(boost_ps[:, c, :], boost_held[:, c : c + 1].to_broadcast([P, P]), ident[:])

        v_codes = sb.tile([P, T], U32, align_bytes=64)
        v_scales = sb.tile([P, T], U8, align_bytes=64)
        v_bf_first = sb.tile([P, QUARTER, PACK], BF16, align_bytes=64)
        interleave(nc.vector.tensor_copy, v_bf_first[:], v_raw[0][:])
        quantize(nc, v_codes[:, 0:QUARTER], v_scales[:, 0:QUARTER], v_bf_first[:])

        boost_sb = sb.tile([P, I], F32)
        nc.scalar.copy(
            boost_sb[:].rearrange("p (n c) -> p n c", c=BOOST_PER_PARTITION), boost_ps[:].rearrange("p c n -> p n c")
        )
        th = sb.tile([P, I], F32)
        b = sb.tile([P, I], F32)
        for h, (slots, entries) in enumerate(zip(slot_halves, list_halves)):
            a_listed = sb.tile([P, I // 2], F32, tag=f"a_listed{h}", align_bytes=64)
            nc.vector.tensor_copy(a_listed[:], a[:].indirect(offsets[:, entries]))
            nc.scalar.activation(th[:, slots], a_listed[:], ACT.Tanh, scale=neg_half_steep[:])
            nc.vector.tensor_scalar(b[:, slots], th[:, slots], -0.5, 0.5, ALU.mult, ALU.add)
        g_bf = sb.tile([P, Q, PACK], BF16, tag="a_listed0", align_bytes=64)
        interleave(nc.vector.tensor_copy, g_bf[:], g_raw[:])
        g_codes = sb.tile([P, Q], U32, align_bytes=64)
        g_scales = sb.tile([P, Q], U8, align_bytes=64)
        quantize(nc, g_codes[:], g_scales[:], g_bf[:])
        nc.vector.tensor_tensor(placed[:].indirect(offsets[:]), b[:], boost_sb[:], ALU.mult)

        v_bf_rest = sb.tile([P, PACK * (T - QUARTER)], BF16, tag="a_listed1", align_bytes=64)
        for c, (lo, hi) in list(enumerate(QUARTERS))[1:]:
            grouped = v_bf_rest[:, PACK * (lo - QUARTER) : PACK * (hi - QUARTER)].rearrange("p (w j) -> p w j", j=PACK)
            interleave(nc.scalar.copy, grouped, v_raw[c][:])
            quantize(nc, v_codes[:, lo:hi], v_scales[:, lo:hi], grouped)

        fac_ps = ps.tile([P, P], F32, tag="spread", bufs=2, name="fac_ps")
        nc.tensor.transpose(fac_ps[:], fac_rows[:], ident[:])
        after_rounding = sb.tile([P, 2 * T + BANK + T // P], F32, tag=f"v_raw{last}")
        c0f_t = after_rounding[:, 0:T]
        neg_s = after_rounding[:, T : 2 * T]
        s_second = after_rounding[:, 2 * T : 2 * T + BANK]
        fac_cols = after_rounding[:, 2 * T + BANK : 2 * T + BANK + T // P]
        nc.scalar.copy(fac_cols, fac_ps[:, 0 : T // P])
        c0f_ps = [ps.tile([P, BANK], F32, tag="c0f", bufs=2, name="c0f_ps") for cols in token_halves]
        for t0 in range(0, T, P):
            block = t0 // P
            c0_t_ps = ps.tile([P, Q], F32, tag=f"bank{block % len(QUARTERS)}", name="c0_t_ps")
            nc.tensor.matmul_mx(
                out=c0_t_ps[:],
                lhsT=v_codes[:, t0 : t0 + P].bitcast(FP8X4),
                lhsT_scale=v_scales[:, t0 : t0 + P],
                rhs=g_codes[:].bitcast(FP8X4),
                rhs_scale=g_scales[:],
                start=True,
                stop=True,
            )
            nc.scalar.activation(c0f_t[:, t0 : t0 + P], c0_t_ps[:], ACT.Copy, scale=fac_cols[:, block : block + 1])
            nc.tensor.transpose(c0f_ps[t0 // BANK][:, t0 % BANK : t0 % BANK + P], c0f_t[:, t0 : t0 + P], ident[:])

        first, second = token_halves
        s_first = sb.tile([P, BANK], F32, tag=f"v_raw{last - 1}")
        neg_max_first = sb.tile([P, 1], F32)
        neg_max = sb.tile([P, 1], F32)
        nc.vector.tensor_tensor(s_first[:], a[:, first], placed[:, first], ALU.add)
        nc.vector.tensor_scalar(neg_s[:, first], s_first[:], -1.0, None, ALU.mult, ALU.min, accum_out=neg_max_first[:])
        nc.vector.tensor_tensor(s_second, a[:, second], placed[:, second], ALU.add)
        nc.vector.tensor_scalar(neg_s[:, second], s_second, -1.0, neg_max_first[:], ALU.mult, ALU.min, accum_out=neg_max[:])

        th_sq = sb.tile([P, I], F32, tag="a")
        nc.gpsimd.tensor_tensor(th_sq[:], th[:], th[:], ALU.mult)
        sigmoid_slope = sb.tile([P, I], F32)
        nc.gpsimd.tensor_scalar(sigmoid_slope[:], th_sq[:], -1.0, neg_steep_scaled[:], ALU.add, ALU.mult)
        slope = sb.tile([P, I], F32)
        nc.gpsimd.tensor_tensor(slope[:], sigmoid_slope[:], boost_sb[:], ALU.mult)

        p = sb.tile([P, T], F32)
        z_first = sb.tile([P, 1], F32)
        z_second = sb.tile([P, 1], F32, tag="z_second")
        shift = sb.tile([P, 1], F32)
        nc.scalar.activation(p[:, first], neg_s[:, first], ACT.Exp, bias=neg_max_first[:], scale=-1.0, accum_out=z_first[:])
        nc.scalar.activation(p[:, second], neg_s[:, second], ACT.Exp, bias=neg_max[:], scale=-1.0, accum_out=z_second[:])
        nc.scalar.activation(shift[:], neg_max_first[:], ACT.Exp, bias=neg_max[:], scale=-1.0)
        z = sb.tile([P, 1], F32)
        nc.scalar.activation(z[:], z_first[:], ACT.Identity, bias=z_second[:], scale=shift[:])

        def weighted_sum(lo, hi, tag):
            products = sb.tile([P, hi - lo], F32, tag=tag, name="products")
            total = sb.tile([P, 1], F32, name=f"total{lo}")
            c0f = c0f_ps[lo // BANK][:, lo % BANK : lo % BANK + hi - lo]
            nc.vector.scalar_tensor_tensor(products[:], c0f, 1.0, p[:, lo:hi], ALU.mult, ALU.mult, accum_out=total[:])
            return total

        sum_first = weighted_sum(0, BANK, "products_first")
        sum_third = weighted_sum(BANK, BANK + QUARTER, "products_third")
        rz = sb.tile([P, 1], F32)
        nc.vector.reciprocal(rz[:], z[:])
        sum_fourth = weighted_sum(BANK + QUARTER, T, "z_second")
        sum_three = sb.tile([P, 1], F32)
        nc.vector.tensor_scalar(sum_three[:], sum_first[:], shift[:], sum_third[:], ALU.mult, ALU.add)
        rz_first = sb.tile([P, 1], F32)
        nc.vector.tensor_scalar(rz_first[:], rz[:], shift[:], None, ALU.mult)
        mean = sb.tile([P, 1], F32)
        nc.vector.tensor_scalar(mean[:], sum_three[:], sum_fourth[:], rz[:], ALU.add, ALU.mult)

        pn = sb.tile([P, T], F32)
        ds = sb.tile([P, T], F32)
        for h, norm in ((1, rz), (0, rz_first)):
            cols = token_halves[h]
            nc.scalar.activation(pn[:, cols], p[:, cols], ACT.Copy, scale=norm[:])
            nc.vector.scalar_tensor_tensor(ds[:, cols], c0f_ps[h][:], mean[:], pn[:, cols], ALU.subtract, ALU.mult)

        ds_listed = sb.tile([P, I], F32)
        nc.vector.tensor_copy(ds_listed[:], ds[:].indirect(offsets[:]))
        nc.vector.tensor_tensor(placed[:].indirect(offsets[:]), ds_listed[:], slope[:], ALU.mult)

        sum_ps = [ps.tile([P, BANK], F32, tag=f"bank{2 + h}", name="sum_ps") for h in range(2)]
        for t0 in range(0, T, P):
            at = t0 % BANK
            nc.tensor.matmul(
                sum_ps[t0 // BANK][:, at : at + P], old_sb[:, t0 : t0 + P], ident[:], start=at == 0, stop=False, is_transpose=True
            )
        ds_scaled = sb.tile([P, T], F32)
        dense_t = sb.tile([P, T], F32)
        res = sb.tile([P, T], F32)
        for h in (1, 0):
            cols = token_halves[h]
            nc.scalar.activation(ds_scaled[:, cols], ds[:, cols], ACT.Copy, scale=OUT_SCALE)
            for at in range(0, BANK, P):
                t0 = h * BANK + at
                nc.tensor.matmul(
                    sum_ps[h][:, at : at + P], ds_scaled[:, t0 : t0 + P], ident[:], start=False, stop=at == BANK - P, is_transpose=True
                )
            nc.scalar.copy(dense_t[:, cols], sum_ps[h][:])
            dense_ps = ps.tile([P, BANK], F32, tag="spread", bufs=2, name="dense_ps")
            for at in range(0, BANK, P):
                t0 = h * BANK + at
                nc.tensor.transpose(dense_ps[:, at : at + P], dense_t[:, t0 : t0 + P], ident[:])

            for at in range(0, BANK, QUARTER):
                piece = slice(h * BANK + at, h * BANK + at + QUARTER)
                if piece.start == BANK:
                    dense_piece = sb.tile([P, QUARTER], F32)
                    nc.scalar.copy(dense_piece[:], dense_ps[:, at : at + QUARTER])
                    nc.gpsimd.tensor_tensor(res[:, piece], dense_piece[:], placed[:, piece], ALU.add)
                    nc.scalar.dma_start(out=out[:, piece], in_=res[:, piece])
                else:
                    nc.vector.tensor_tensor(res[:, piece], dense_ps[:, at : at + QUARTER], placed[:, piece], ALU.add)
                    nc.sync.dma_start(out=out[:, piece], in_=res[:, piece])
